import numpy as np, ml_dtypes
CORES = [36,164,52,180,100,228,116,244]
N = 8
import mx_ref
BF = ml_dtypes.bfloat16
def entries(a):
    return np.ascontiguousarray(a.T).reshape(-1)
def table(e):
    return np.ascontiguousarray(np.reshape(e, (-1, 16)).T).astype(np.int32)
def pick(q, e):
    c = np.concatenate([q[0].reshape(128, -1, 4), np.zeros((128, 1, 4), np.uint8)], axis=1); s = np.concatenate([q[1], np.ones((16, 1), np.uint8)], axis=1)
    return (np.ascontiguousarray(c[:, e].reshape(128, -1)), np.ascontiguousarray(s[:, e]))
def join(*qs):
    return (np.concatenate([q[0] for q in qs], axis=1), np.concatenate([q[1] for q in qs], axis=1))
def put(q, e, v):
    c, s = q[0].reshape(128, -1, 4).copy(), q[1].copy(); c[:, e] = v[0].reshape(128, -1, 4); s[:, e] = v[1]
    return (c.reshape(128, -1), s)
def pk(c, s):
    return (np.ascontiguousarray(c), mx_ref.live(s))
def emit(q):
    return q[0], q[1]
def cols(t, e):
    v = np.concatenate([t.reshape(128, -1, 4), np.zeros((128, 1, 4), BF)], axis=1)
    return np.ascontiguousarray(v[:, e]).reshape(128, -1)
def cut(t, i, w=512):
    return t[:, w * i:w * i + w]
def f(rng, *shape):
    return mx_ref.flush((rng.standard_normal(shape, dtype=np.float32) * np.exp2(rng.integers(-2, 3, shape[:-1] + (1,)))).astype(BF))
def wide(rng, *shape, cols=0):
    v = rng.standard_normal(shape, dtype=np.float32) * np.exp2(rng.integers(-12, 13, shape)).astype(np.float32)
    if cols: v *= np.repeat(np.exp2(rng.integers(-cols, cols + 1, shape[:-2] + (1, shape[-1] // 4))) * (rng.random(shape[:-2] + (1, shape[-1] // 4)) > 0.0625), 4, axis=-1).astype(np.float32)
    return mx_ref.flush(v.astype(BF))
P, CAPP, LC = 128, 16, 64
def choose(e, g, d):
    c = e[np.arange(P), np.argmax(g[e], axis=1)]
    for s in range(N):
        if s != d:
            late = np.flatnonzero(c // P == s)[CAPP:]
            c[late] = e[late, 0]
    return c
def play(e0, e1, e2, p1, p2, u, a):
    k = [mx_ref.quantize(u[d]) for d in range(N)]
    A = [[mx_ref.quantize(np.ascontiguousarray(cut(a[d], i))) for i in range(4)] for d in range(N)]
    H = [mx_ref.quantize(e0[d]) for d in range(N)]
    g = np.stack([mx_ref.matmul(k[d], H[d])[0] for d in range(N)]) + np.float32(0)
    chosen, tiles, scores = [], [], [g]
    for e, p in ((e1, p1), (e2, p2)):
        every, before = join(*H), g.reshape(-1)
        H, g = [], np.zeros((N, P), np.float32)
        for d in range(N):
            c = choose(entries(p[d]).reshape(P, 4), before, d)
            x = pick(every, c)
            R = np.stack([mx_ref.matmul(A[d][i], x) for i in range(4)], axis=2).reshape(128, 4 * P)
            h = (R * np.float32(0.05) + e[d].astype(np.float32)).astype(BF)
            q = mx_ref.quantize(h)
            g[d] = before[c] + mx_ref.matmul(k[d], q)[0]
            H.append(q)
            chosen.append(c)
            tiles.append(h)
        scores.append(g)
    return np.stack(chosen).reshape(2, N, P), tiles, scores, H
def large(v):
    v = v.astype(np.float32)
    v[np.abs(v) < np.float32(0.03125)] = 0
    return v.astype(BF)
def lean(v, u, s):
    t = np.abs(v.astype(np.float32)).reshape(128, -1, 4) * np.sign(u[:, None, :4].astype(np.float32)) * np.asarray(s, np.float32)[None, :, None]
    return t.reshape(128, -1).astype(BF)
def near(t, u, score):
    size = np.concatenate([[0.0], np.exp2(np.arange(-26, -7))])[:, None] * np.array([1, 1.25, 1.5, 1.75])
    v = np.repeat(t.astype(np.float32).reshape(128, 1, 4), 80, axis=1)
    v[:8] = np.sign(u[:8, None, :4].astype(np.float32)) * size.reshape(1, 80, 1)
    v = np.ascontiguousarray(v.reshape(128, 320).astype(BF))
    s = score(v)
    i = int(np.argmin(np.abs(s - s[0] - np.float32(2.5) * np.spacing(np.abs(s[0])))))
    return cols(v, [0, i])
def strong(u):
    return (u.astype(np.float32) * np.float32(2.0 ** 24)).astype(BF)
def lists(rng):
    out = []
    for d in range(N):
        others = np.delete(np.arange(N), d)
        rank = others[np.argsort(rng.random((P, N - 1)), axis=1)[:, :3]]
        pool = np.stack([rng.permutation(P)[:LC] for s in range(N)])
        e = np.zeros((P, 4), int)
        e[:, 0] = d * P + rng.integers(0, P, P)
        e[:, 1:] = rank * P + pool[rank, rng.integers(0, LC, (P, 3))]
        out.append(table(e.reshape(-1)))
    return np.stack(out)
def crowd(rng, s):
    out, half = [], LC // 2
    for d in range(N):
        x = rng.permutation(np.delete(np.arange(N), d))
        hi = np.stack([rng.permutation(np.flatnonzero(s[r]))[:half] for r in range(N)])
        lo = np.stack([rng.permutation(np.flatnonzero(~s[r]))[:half] for r in range(N)])
        j = rng.permutation(P)
        one, two, home = j[:P // 2], j[P // 2:P // 2 + CAPP], j[P // 2 + CAPP:]
        rank = np.stack([np.full(P, x[0]), np.full(P, x[1]), x[rng.integers(2, N - 1, P)]], axis=1)
        n = rng.integers(0, half, (P, 3))
        n[j, 0] = np.arange(P) % (P // 2) % half
        n[two, 1] = rng.permutation(half)[:CAPP]
        at = lo[rank, n]
        at[one, 0] = hi[x[0], n[one, 0]]
        at[two, 1] = hi[x[1], n[two, 1]]
        e = np.zeros((P, 4), int)
        e[:, 0] = d * P + np.flatnonzero(~s[d])[rng.integers(0, P // 2, P)]
        e[home, 0] = d * P + np.flatnonzero(s[d])[rng.integers(0, P // 2, home.size)]
        e[:, 1:] = rng.permuted(rank * P + at, axis=1)
        out.append(table(e.reshape(-1)))
    return np.stack(out)
def plain(rng):
    u = np.array(f(rng, 128, 512))
    u[:, 4:] = 0
    return {"e0": np.array(f(rng, N, 128, 4 * P)), "e1": large(f(rng, N, 128, 4 * P)), "e2": large(f(rng, N, 128, 4 * P)), "p1": lists(rng), "p2": lists(rng),
            "u": np.stack([u] * N), "a": f(rng, N, 128, 2048), "w": f(rng, N, 128, 512)}
def setup_inputs(rng):
    return plain(rng)
def setup_inputs_full(rng):
    d = plain(rng)
    for e, p, size in (("e0", "p1", 1), ("e1", "p2", 64)):
        s = np.stack([rng.permutation(P) < P // 2 for r in range(N)])
        for r in range(N): d[e][r] = lean(d[e][r], d["u"][r], size * np.where(s[r], 1, -1))
        d[p] = crowd(rng, s)
    return d
def setup_inputs_ties(rng):
    d = plain(rng)
    u, a = np.ascontiguousarray(d["u"][0]), np.array(d["a"][0])
    a.reshape(128, 4, 512)[:, :, :32] = 0
    k = mx_ref.quantize(u)
    def row(t): return mx_ref.matmul(k, mx_ref.quantize(t))[0]
    x = np.concatenate([f(rng, 128, 16), near(lean(f(rng, 128, 4), u, [1]), u, row)], axis=1)
    best = cols(x, [5] * 4)
    top, q = row(best)[0], mx_ref.quantize(best)
    R = np.stack([mx_ref.matmul(mx_ref.quantize(np.ascontiguousarray(cut(a, i))), q)[:, 0] for i in range(4)], axis=1)
    def later(t): return top + row((np.tile(R, 80) * np.float32(0.05) + t.astype(np.float32)).astype(BF))
    z = near(lean(large(f(rng, 128, 4)), u, [8]), u, later)
    d["e0"] = np.stack([cols(x, rng.integers(0, 6, P)) for r in range(N)])
    d["e1"] = np.stack([cols(z, rng.integers(0, 2, P)) for r in range(N)])
    d["a"] = np.stack([a] * N)
    return d
def setup_inputs_own(rng):
    d = plain(rng)
    d["u"] = strong(d["u"])
    best, worst = rng.permutation(N)[:2]
    for r, s in ((best, 1), (worst, -1)):
        d["e0"][r] = lean(d["e0"][r], d["u"][r], np.full(P, 8 * s))
        d["e1"][r] = lean(d["e1"][r], d["u"][r], np.full(P, 256 * s))
    return d
def setup_inputs_flip(rng):
    d = plain(rng)
    d["u"] = strong(d["u"])
    for r in range(N):
        s = rng.permutation(P) % 2 * 2 - 1
        d["e0"][r] = lean(d["e0"][r], d["u"][r], 1024 * s)
        d["e1"][r] = lean(d["e1"][r], d["u"][r], -16384 * s)
    return d
def setup_inputs_spread(rng):
    d = plain(rng)
    d["e0"] = wide(rng, N, 128, 4 * P, cols=4)
    d["e1"] = large(wide(rng, N, 128, 4 * P, cols=4))
    d["e2"] = large(wide(rng, N, 128, 4 * P, cols=4))
    return d
def check_inputs(d):
    b = []
    for k in ("e0", "e1", "e2", "u", "a", "w"):
        v = np.abs(d[k].astype(np.float32))
        if not (np.isfinite(v).all() and ((v == 0) | (v >= 2.0 ** -30) & (v <= 2.0 ** 30)).all()): b.append("a value of " + k)
    u = d["u"].astype(np.float32)
    if (u[:, :, 4:] != 0).any(): b.append("u has numbers behind its column 0")
    if (u != u[:1]).any(): b.append("u isn't the same on all ranks")
    for k in ("p1", "p2"):
        for r in range(N):
            e = entries(d[k][r]).reshape(P, 4)
            if e.min() < 0 or e.max() >= N * P:
                b.append(k + " out of range")
                continue
            o = np.sort(e[:, 1:] // P, axis=1)
            if (e[:, 0] // P != r).any(): b.append(k + ": predecessor 0")
            if (o == r).any() or (o[:, 1:] == o[:, :-1]).any(): b.append(k + ": predecessors 1 to 3")
            if np.bincount(np.unique(e[:, 1:]) // P, minlength=N).max() > LC: b.append(k + ": too many columns of one rank")
    if not b:
        chosen, tiles, scores, H = play(*[d[k] for k in ("e0", "e1", "e2", "p1", "p2", "u", "a")])
        v = np.abs(np.stack(tiles).astype(np.float32))
        if not (np.isfinite(v).all() and ((v == 0) | (v >= 2.0 ** -30) & (v <= 2.0 ** 30)).all()): b.append("a value of h_1 or h_2")
        if not np.isfinite(np.stack(scores)).all(): b.append("a score")
    return b
def reference(e0, e1, e2, p1, p2, u, a, w):
    chosen, tiles, scores, H = play(e0, e1, e2, p1, p2, u, a)
    ch, g = np.zeros((N, 2, P), np.float32), np.zeros((N, 1, P), np.float32)
    oc, osc, y = np.zeros((N, 128, 4 * P), np.uint8), np.zeros((N, 16, P), np.uint8), np.zeros((N, 128, P), np.float32)
    for r in range(N):
        ch[r] = chosen[:, r]
        g[r, 0] = scores[2][r]
        oc[r], osc[r] = emit(H[r])
        y[r] = mx_ref.matmul(mx_ref.quantize(w[r]), H[r])
    return {"ch": ch, "g": g, "oc": oc, "osc": osc, "y": y}

@@ -1,0 +1,453 @@
+from concourse.bass import DstId, RemoteDMATransfer
+from concourse.mybir import dt, AluOpType, ActivationFunctionType
+
+X4 = "float8_e4m3fn_x4"
+F, B, I, U16, U8 = "float32", "bfloat16", "int32", "uint16", "uint8"
+
+
+def _sb(n, d):
+    return ("sbuf", [128, n], d)
+
+
+SCRATCH = {
+    "e0t": _sb(512, B), "e1t": _sb(512, B), "e2t": _sb(512, B), "at": _sb(2048, B), "wt": _sb(512, B), "ut": _sb(4, B),
+    "ubig": _sb(512, B),
+    "pst": ("dram", [128, 4], I), "pl": ("dram", [8, 128, 4], I),
+    "l1": _sb(32, I), "lo": _sb(32, I), "l2": _sb(32, I),
+    "uq": _sb(128, X4), "us": _sb(128, U8), "aq": _sb(512, X4), "asc": _sb(512, U8), "wq": _sb(128, X4), "ws": _sb(128, U8),
+    "hall": _sb(1024, X4), "halls": _sb(1024, U8), "x1": _sb(128, X4), "x1s": _sb(128, U8),
+    "h1q": _sb(128, X4), "h1s": _sb(128, U8), "pk": _sb(128, X4), "pks": _sb(128, U8),
+    "win2": _sb(256, X4), "win2s": _sb(256, U8), "x2": _sb(128, X4), "x2s": _sb(128, U8),
+    "h2q": _sb(128, X4), "h2s": _sb(128, U8),
+    "ones": _sb(128, B), "hold32": _sb(512, B), "hold16": _sb(128, B), "rst": _sb(512, F), "pidx": _sb(1, I), "r15": _sb(1, I),
+    "r31": _sb(1, I), "ip": _sb(1, F), "sp31": _sb(1, F), "spx": _sb(1, F), "spart": _sb(1, F), "cmod": _sb(128, I),
+    "mask16": _sb(128, B), "ci": _sb(128, I), "repo": _sb(40, U16), "rsh": _sb(40, I), "dupo": _sb(16, U16),
+    "io1": _sb(1024, F), "eidx": _sb(512, F),
+    "off1": _sb(32, U16), "offo": _sb(32, U16), "offh": _sb(16, U16), "off2": _sb(32, U16), "er": _sb(512, F), "er2": _sb(512, F),
+    "kt": _sb(512, F), "kp": _sb(256, F), "key1": _sb(256, F), "key2": _sb(512, F), "st1": _sb(256, F),
+    "ew": _sb(128, F), "es": _sb(128, F), "ew2": _sb(128, F), "es2": _sb(128, F),
+    "sc": _sb(1024, F), "gv": _sb(512, F), "mx": _sb(512, F), "pm": _sb(512, B), "st": _sb(512, F),
+    "zb1": _sb(128, I), "zf1": _sb(128, F), "zi2": _sb(128, I), "zb2": _sb(128, I), "zrow": _sb(128, F), "zf2": _sb(128, F),
+    "sj": _sb(128, I), "mk": _sb(128, B), "th": _sb(128, B), "cum": _sb(128, B), "cs": _sb(128, F),
+    "dup1": _sb(256, B), "dup2": _sb(256, B), "v2": _sb(256, B), "vt": _sb(256, B), "vs": _sb(256, B),
+    "f8": _sb(160, F), "i8": _sb(32, I), "cu1": _sb(8, U16), "cu2": _sb(8, U16),
+    "base1": _sb(128, F), "bt": _sb(128, F), "gt": _sb(128, F), "sp": _sb(32, F), "d1": _sb(512, F), "rp": _sb(1024, F),
+    "sc2": _sb(1024, F), "base2": _sb(128, F), "gout": _sb(128, F), "yt": _sb(128, F),
+    "am": _sb(128, I), "mb": _sb(144, B), "ce": _sb(128, B), "pp": _sb(128, B), "ks": _sb(128, F), "lr": _sb(32, F),
+    "lt": _sb(32, F), "ls": _sb(128, F), "r8i": _sb(8, I), "r8n": _sb(8, I), "offp": _sb(8, U16),
+    "ixu": _sb(8, U16), "chr1": _sb(128, F), "chr2": _sb(128, F),
+    "hs1": _sb(512, F), "hs2": _sb(512, F), "h1": _sb(512, B), "h2": _sb(512, B),
+    "ps": ("psum", [128, 2048], F), "pr": ("psum", [128, 2048], F),
+}
+
+REMOTE = ["al", "a0a", "a0b", "a0h", "ae", "a2", "left", "hl", "hc", "kc", "ks"]
+SEMAPHORES = REMOTE + ["v"] + ["s%d" % i for i in range(138)]
+A = AluOpType
+CP, IDN = ActivationFunctionType.Copy, ActivationFunctionType.Identity
+TOP = 2.0 ** 19
+
+TIERS = (("a0a", {1: 2, 2: 2, 3: 2, 4: 2}), ("a0b", {5: 4, 6: 4}))
+TIER_H = ("a0h", {7: 8})
+LISTS = ({1: 2, 2: 2, 3: 2, 4: 2}, {5: 2, 6: 2, 7: 4})
+SCORES = {q: 1 for q in range(1, 8)}
+PICKS, PICKS_H = {1: 2, 2: 2, 3: 4}, ({4: 4, 5: 4}, {6: 4, 7: 4})
+
+
+def helpers(core, topo):
+    return [c for c in topo.cores_of(core) if topo.die(c) != topo.die(core)][:len(LISTS)]
+
+
+def fused(g, T, topo, core, parts):
+    tr = []
+    for c, e, sem, src, dst in parts:
+        rid, pid = topo.addr(c, core)
+        tr.append(RemoteDMATransfer(dst_ids=[DstId(rid=rid, pnc=pid)], dma_engine_mask=sum(1 << x for x in e), remote_sem=T.sem[sem],
+                                    srcs=[src], dsts=[dst]))
+    g.remote_dma_fused(tr, local_sem=T.sem.left)
+    return sum(len(e) for c, e, sem, src, dst in parts)
+
+
+def far(T, topo, core, me, share, sem, src, dst):
+    parts, at = [], 0
+    for q, n in share.items():
+        d = (me + q) % len(T.cores)
+        parts.append((T.cores[d], topo.engines(core, T.cores[d])[at:at + n], sem, src(q), dst(d)))
+        at += n
+    return parts
+
+
+def inner(T, topo, core, me):
+    away = topo.engines(core, T.cores[(me + 1) % len(T.cores)])
+    return [x for x in topo.engines(core, helpers(core, topo)[0]) if x not in away]
+
+
+def near(T, topo, core, me, sem, src, n=None):
+    hp, e = helpers(core, topo), inner(T, topo, core, me)
+    m = len(e) // len(hp)
+    return [(c, e[m * i:m * i + (n or m)], sem, src(i), src(i)) for i, c in enumerate(hp)]
+
+
+def columns0(T, me):
+    mine = slice(128 * me, 128 * me + 128)
+    return T.hall[:, mine].bitcast(dt.uint8), T.halls[:, mine]
+
+
+def pick_calls(T, me):
+    land = slice(16 * me, 16 * me + 16)
+    return (("kc", lambda q: T.pk[:, 16 * q:16 * q + 16].bitcast(dt.uint8), lambda d: T.win2[:, land].bitcast(dt.uint8)),
+            ("ks", lambda q: T.pks[:, 16 * q:16 * q + 16], lambda d: T.win2s[:, land]))
+
+
+def helper_program(g, core, T, topo, me, k):
+    N, own = len(T.cores), T.cores[me]
+    g.wait_ge(T.sem.hl, 1)
+    left = fused(g, T, topo, core, far(T, topo, core, me, LISTS[k], "al", lambda q: T.pst[:], lambda d: T.pl[(me - d) % N]))
+    g.wait_ge(T.sem.hc, len(inner(T, topo, own, me)))
+    piece = columns0(T, me)[k]
+    left += fused(g, T, topo, core, far(T, topo, core, me, TIER_H[1], TIER_H[0], lambda q: piece, lambda d: piece))
+    n = len(near(T, topo, own, me, "kc", lambda i: None)[k][1])
+    for sem, src, dst in pick_calls(T, me):
+        g.wait_ge(T.sem[sem], n)
+        left += fused(g, T, topo, core, far(T, topo, core, me, PICKS_H[k], "a2", src, dst))
+    g.wait_ge(T.sem.left, left)
+
+
+def rank_program(g, core, T, topo):
+    me = T.rank_of(core)
+    if me is None:
+        for r, c in enumerate(T.cores):
+            if core in helpers(c, topo):
+                helper_program(g, core, T, topo, r, helpers(c, topo).index(core))
+        return
+    N = len(T.cores)
+    Q = {"g": g, "v": g.vector, "s": g.scalar, "t": g.tensor, "y": g.sync}
+    total, seen, used = {"left": 0}, {}, [0]
+
+    def wait(q, deps):
+        for sem in deps:
+            assert sem != "v" or q == "v"
+            if seen.get((q, sem), 0) < total.get(sem, 0):
+                Q[q].wait_ge(T.sem[sem], total[sem])
+                seen[(q, sem)] = total[sem]
+
+    def fresh():
+        used[0] += 1
+        return "s%d" % (used[0] - 1)
+
+    def mark(q, ins, n, cross, sem=None):
+        if sem is None:
+            sem = "v" if q == "v" and not cross else fresh()
+        total[sem] = total.get(sem, 0) + n
+        ins.then_inc(T.sem[sem], n)
+        return sem
+
+    def dma(q, out, in_, deps=(), sem=None):
+        wait(q, deps)
+        return mark(q, Q[q].dma_start(out, in_), 16, True, sem)
+
+    F_ = {"copy": g.vector.tensor_copy, "tt": g.vector.tensor_tensor, "ts": g.vector.tensor_scalar, "set": g.vector.memset,
+          "scan": g.vector.tensor_tensor_scan, "tr": g.vector.transpose, "quant": g.vector.quantize_mx,
+          "mm": g.tensor.matmul_mx, "act": g.scalar.activation, "iota": g.iota, "bc": g.partition_broadcast}
+
+    def op(q, name, args, deps=(), cross=True, sem=None, **kw):
+        wait(q, deps)
+        return mark(q, F_[name](*args, **kw), 1, cross, sem)
+
+    def v(name, *args, deps=("v",), cross=False, sem=None):
+        return op("v", name, args, deps, cross, sem)
+
+    def send(parts, deps):
+        wait("g", deps)
+        total["left"] += fused(g, T, topo, core, parts)
+
+    def count(*shares):
+        return sum(n for share in shares for n in share.values())
+
+    total["al"], total["ae"], total["a2"] = count(*LISTS), count(SCORES), 2 * count(PICKS, *PICKS_H)
+    for sem, share in TIERS + (TIER_H,):
+        total[sem] = 2 * count(share)
+    arrivals = [sem for sem, share in TIERS + (TIER_H,)]
+    mine = slice(128 * me, 128 * me + 128)
+    halves = slice(0, 64), slice(64, 128)
+    two = {name: (fresh(), fresh()) for name in ("scan", "mark", "key", "whole", "rank")}
+
+    ld_e0 = dma("y", T.e0t[:], T.e0[:])
+    ld_ps = dma("s", T.pst[:], T.p2[:])
+    ld_u = dma("s", T.ut[:], T.u[:, 0:4])
+    ld_own = dma("s", T.pl[0], T.p2[:])
+    ld_l1, ld_lo = None, None
+    for k in range(8):
+        ld_l1 = dma("y", T.l1[16 * k:16 * k + 16, :], T.p1[:], (), ld_l1)
+    for k in range(8):
+        ld_lo = dma("y", T.lo[16 * k:16 * k + 16, :], T.p2[:], (), ld_lo)
+    wait("y", arrivals[:1])
+    ld_a = dma("y", T.at[:], T.a[:])
+    wait("y", arrivals)
+    ld_e1 = dma("y", T.e1t[:], T.e1[:])
+    ld_l2 = dma("y", T.l2[:], T.pl[:], ("al", ld_own))
+    ld_w = dma("y", T.wt[:], T.w[:])
+    ld_e2 = dma("y", T.e2t[:], T.e2[:])
+
+    i_p = op("g", "iota", (T.pidx[:], [[0, 1]], 0, 1))
+    i_0 = op("g", "iota", (T.io1[:, 0:128], [[1, 128]], 0, 0), allow_small_or_imprecise_dtypes=True)
+    i_1 = fresh()
+    for k in range(1, 8):
+        op("s", "act", (T.io1[:, 128 * k:128 * k + 128], T.io1[:, 0:128], IDN), (i_0,), sem=i_1, bias=float(128 * k))
+
+    send(near(T, topo, core, me, "hl", lambda i: T.pst[:], 1), (ld_ps,))
+    x_h0 = v("quant", T.hall[:, mine], T.halls[:, mine], T.e0t[:], deps=(ld_e0,), cross=True)
+    for sem, share in TIERS:
+        if sem == TIERS[1][0]:
+            for c, piece in zip(helpers(core, topo), columns0(T, me)):
+                send([(c, inner(T, topo, core, me), "hc", piece, piece)], (x_h0,))
+        for piece in columns0(T, me):
+            send(far(T, topo, core, me, share, sem, lambda q: piece, lambda d: piece), (x_h0,))
+
+    v("set", T.ones[:], 1.0)
+    v("ts", T.r15[:], T.pidx[:], 15, None, A.bitwise_and, deps=(i_p,))
+    v("ts", T.r31[:], T.pidx[:], 31, None, A.bitwise_and, deps=())
+    v("copy", T.ci[:], T.io1[:, 0:128], deps=(i_0,))
+    for buf, c in ((T.hold32[:, 0:256], 1.0), (T.hold16[:], 1.0), (T.rst[:, 0:256], 0.0), (T.pm[:, 0:512:4], 1.0), (T.mb[:, 0:1], 0.0)):
+        v("set", buf, c, deps=())
+    s_e = op("s", "act", (T.eidx[:], T.io1[:, 0:512], CP), (i_1,), scale=1024.0 / TOP)
+
+    for a in range(2):
+        v("copy", T.offh[64 * a:64 * a + 64, :], T.l1[64 * a:64 * a + 64, 16 * a:16 * a + 16], deps=(ld_l1,))
+    v("copy", T.off1[:], T.l1[:], deps=())
+    for t in range(4):
+        v("ts", T.ubig[:, t:512:4], T.ones[:], T.ut[:, t:t + 1], None, A.mult, deps=("v", ld_u) if t == 0 else ())
+    x_off1 = v("copy", T.ip[:], T.r15[:], cross=True)
+    s_kp = op("s", "act", (T.kp[:], T.io1[:].indirect(T.offh[:]), CP), (x_off1, i_1), scale=1.0 / TOP)
+    s_er = op("s", "act", (T.er[:], T.io1[:].indirect(T.off1[:]), CP))
+    x_u = v("quant", T.uq[:], T.us[:], T.ubig[:], deps=("v",), cross=True)
+    v("set", T.hold32[:, 0:256:32], 0.0, deps=())
+    v("set", T.hold16[:, 0:128:16], 0.0, deps=())
+    v("set", T.rst[:, 0:256:4], -1.0e29, deps=())
+    v("copy", T.sp31[:], T.r31[:], deps=())
+    v("ts", T.cmod[:], T.ci[:], 15, None, A.bitwise_and, deps=())
+    v("ts", T.rsh[:], T.ci[:, 0:40], 1, None, A.logical_shift_right, deps=())
+    v("ts", T.spx[:], T.sp31[:], float(me), 99.0, A.is_equal, A.mult, deps=("v", x_off1))
+    v("ts", T.mask16[:], T.cmod[:], T.ip[:], None, A.is_equal, deps=())
+    v("ts", T.dupo[:], T.rsh[:, 0:16], 16.0, T.ip[:], A.mult, A.add, deps=())
+    x_rep = v("ts", T.repo[:], T.rsh[:], 12.0, None, A.add, deps=(), cross=True)
+    v("tt", T.spart[:], T.spx[:], T.sp31[:], A.add)
+    for a in range(2):
+        h = slice(64 * a, 64 * a + 64)
+        v("tt", T.key1[h, :], T.kp[h, :], T.eidx[h, 256 * a:256 * a + 256], A.add, deps=(s_kp, s_e))
+
+    def e0table(ew, es, row, deps):
+        v("tt", ew[:], row[:, 0:512:4], T.mask16[:], A.mult, deps=deps)
+        v("scan", es[:], T.hold16[:], ew[:], 0.0, A.mult, A.add)
+
+    x_offo = v("copy", T.offo[:], T.lo[:], deps=(ld_lo,), cross=True)
+    s_er2 = op("s", "act", (T.er2[:], T.io1[:].indirect(T.offo[:]), CP), (x_offo,))
+    e0table(T.ew, T.es, T.er, ("v", s_er))
+    v("set", T.d1[:], 0.0, deps=())
+    v("set", T.hold32[:, 256:512], 1.0, deps=())
+    v("set", T.rst[:, 256:512], 0.0, deps=())
+    v("set", T.hold32[:, 256:512:32], 0.0)
+    v("set", T.rst[:, 256:512:4], -1.0e29, deps=())
+    e0table(T.ew2, T.es2, T.er2, ("v", s_er2))
+
+    sc_done = []
+    order = [(me, x_h0)] + [((me - q) % N, sem) for sem, share in (TIERS[0], TIER_H, TIERS[1]) for q in share]
+    for i, (r, sem) in enumerate(order):
+        cs = slice(128 * r, 128 * r + 128)
+        bank = (T.ps if i < 4 else T.pr)[:, 512 * (i % 4):512 * (i % 4) + 128]
+        m = op("t", "mm", (bank, T.uq[:], T.us[:], T.hall[:, cs], T.halls[:, cs], True, True), (x_u, sem))
+        if i % 2:
+            sc_done.append(v("copy", T.sc[:, cs], bank, deps=(m,), cross=True))
+        else:
+            sc_done.append(op("s", "act", (T.sc[:, cs], bank, CP), (m,)))
+    arrived = [x_h0] + arrivals
+
+    def choose(w, parts, key, st):
+        h = w // 2
+        for i in range(2):
+            c = slice(h * i, h * i + h)
+            v("scan", T.mx[:, c], T.rst[:, c], T.gv[:, c], 0.0, A.add, A.max, deps=(parts[i],), sem=two["scan"][i])
+        for i in range(2):
+            for k in (1, 2, 3):
+                a, e = h * i + k, h * i + h
+                v("tt", T.pm[:, a:e:4], T.gv[:, a:e:4], T.mx[:, a - 1:e:4], A.is_gt, deps=(two["scan"][i],), sem=two["mark"][i])
+        for i in range(2):
+            c = slice(h * i, h * i + h)
+            v("scan", st[:, c], T.pm[:, c], key[:, c], 0.0, A.max, A.min, deps=(two["mark"][i],), sem=two["key"][i])
+        return two["key"]
+
+    def f8(i):
+        return T.f8[:, 8 * i:8 * i + 8]
+
+    def i8(i):
+        return T.i8[:, 8 * i:8 * i + 8]
+
+    etab, etab2, cnt = T.es[:, 15:128:16], T.es2[:, 15:128:16], T.vs[:, 31:256:32]
+
+    def quant_a(i):
+        return v("quant", T.aq[:, 128 * i:128 * i + 128], T.asc[:, 128 * i:128 * i + 128], T.at[:, 512 * i:512 * i + 512], deps=(ld_a,),
+                 cross=True)
+
+    def update(hs, h, X, Xs, e, ld_e, deps, x_a, between=None):
+        dep = []
+        for i in range(4):
+            s = slice(128 * i, 128 * i + 128)
+            m = op("t", "mm", (T.pr[:, 512 * i:512 * i + 128], T.aq[:, s], T.asc[:, s], X[:], Xs[:], True, True), tuple(deps) + (x_a[i],))
+            dep.append(op("s", "act", (hs[:, s], T.pr[:, 512 * i:512 * i + 128], CP), (m,), scale=0.05))
+        if between:
+            between()
+        for i in range(4):
+            v("tt", h[:, i:512:4], hs[:, 128 * i:128 * i + 128], e[:, i:512:4], A.add, deps=(dep[i], ld_e))
+
+    x_g1 = v("copy", T.gv[:, 0:128], T.sc[:].indirect(T.offh[:, 0:8]), deps=["v"] + sc_done, cross=True)
+    s_g1 = op("s", "act", (T.gv[:, 128:256], T.sc[:].indirect(T.offh[:, 8:16]), CP), sc_done)
+    x_st1 = choose(256, (x_g1, s_g1), T.key1, T.st1)
+    s_zf = fresh()
+    for a, to in enumerate(halves):
+        for there in halves:
+            v("ts", T.zb1[there, to], T.st1[to, 3:256:4], TOP, None, A.mult, deps=x_st1, sem=two["whole"][a])
+            op("s", "act", (T.zf1[there, to], T.st1[to, 3:256:4], CP), x_st1, sem=s_zf)
+
+    for i, c in enumerate(halves):
+        v("ts", T.sj[:, c], T.zb1[:, c], 7, 7, A.logical_shift_right, A.bitwise_and, deps=(two["whole"][i],), sem=two["rank"][i])
+    x_th = fresh()
+    for i, c in enumerate(halves):
+        v("ts", T.th[:, c], T.sj[:, c], T.spart[:], 1.0e6, A.not_equal, A.mult, deps=(two["rank"][i],), sem=x_th)
+    s_th = op("s", "act", (T.dup1[:], T.th[:].indirect(T.dupo[:]), CP), (x_th,))
+    v("ts", T.mk[:], T.sj[:], T.spart[:], None, A.is_equal, deps=())
+    x_cum1 = v("scan", T.cum[:], T.ones[:], T.mk[:], -16.5, A.mult, A.add, cross=True)
+    x_cs1 = v("scan", T.cs[:], T.mask16[:], T.zf1[:], 0.0, A.max, A.min, deps=(s_zf,), cross=True)
+    x_a = [quant_a(0)]
+    x_v1 = v("tt", T.v2[:], T.cum[:].indirect(T.dupo[:]), T.dup1[:], A.is_gt, deps=(x_cum1, s_th), cross=True)
+    x_i0 = v("ts", i8(0), T.cs[:, 15:128:16], TOP, None, A.mult, deps=(x_cs1,), cross=True)
+    x_vt = v("tr", T.vt[:], T.v2[:], deps=(x_v1,), cross=True)
+    x_i1 = v("ts", i8(1), i8(0), 1023, None, A.bitwise_and, deps=(x_i0,), cross=True)
+    v("scan", T.vs[:], T.hold32[:, 0:256], T.vt[:], 0.0, A.mult, A.add, deps=(x_vt,))
+    v("tt", f8(0), etab, i8(1), A.subtract, deps=(x_i1,))
+    v("tt", f8(1), cnt, f8(0), A.mult)
+    v("tt", f8(2), f8(1), i8(1), A.add)
+    x_c1 = v("copy", T.cu1[:], f8(2), cross=True)
+
+    s_x1 = op("s", "act", (T.x1s[:], T.halls[:].indirect(T.cu1[:]), CP), [x_c1] + arrived)
+    s_b1 = op("s", "act", (T.base1[:], T.sc[:].indirect(T.cu1[:]), CP))
+    x_x1 = v("copy", T.x1[:].bitcast(dt.uint32), T.hall[:].bitcast(dt.uint32).indirect(T.cu1[:]), deps=[x_c1] + arrived, cross=True)
+    x_a += [quant_a(i) for i in (1, 2, 3)]
+    update(T.hs1, T.h1, T.x1, T.x1s, T.e1t, ld_e1, (x_x1, s_x1), x_a)
+    x_h1 = v("quant", T.h1q[:], T.h1s[:], T.h1[:], cross=True)
+
+    m = op("t", "mm", (T.ps[:, 0:128], T.uq[:], T.us[:], T.h1q[:], T.h1s[:], True, True), (x_h1,))
+    x_off2 = v("copy", T.off2[:], T.l2[:], deps=(ld_l2,), cross=True)
+    s_kt = op("s", "act", (T.kt[:], T.io1[:].indirect(T.off2[:]), CP), (x_off2,), scale=1.0 / TOP)
+    v("tr", T.bt[:], T.base1[:], deps=(s_b1,))
+    v("tr", T.gt[:], T.ps[:, 0:128], deps=(m,))
+    x_sp = v("tt", T.sp[:, 4 * me:4 * me + 4], T.gt[:, 0:128:32], T.bt[:, 0:128:32], A.add, cross=True)
+    own_sp = T.sp[:, 4 * me:4 * me + 4]
+    send(far(T, topo, core, me, SCORES, "ae", lambda q: own_sp, lambda d: own_sp), (x_sp,))
+
+    v("quant", T.win2[:, 128:256], T.win2s[:, 128:256], T.h1[:], deps=())
+    x_w = v("quant", T.wq[:], T.ws[:], T.wt[:], deps=(ld_w,), cross=True)
+    v("tt", T.key2[:], T.kt[:], T.eidx[:], A.add, deps=(s_kt, s_e))
+    x_ch1 = v("copy", T.chr1[:], T.io1[:].indirect(T.cu1[:]), deps=(x_c1, i_1), cross=True)
+    dma("y", T.ch[0:1, :], T.chr1[0:1, :], (x_ch1,))
+
+    v("copy", T.d1[:, 0:384:32], T.sp[:, 0:12], deps=("v", "ae", x_sp))
+    s_rp = [op("s", "act", (T.rp[:, 384:640], T.sp[:].indirect(T.repo[:, 0:16]), CP), ("ae", x_sp, x_rep)),
+            op("s", "act", (T.rp[:, 640:1024], T.sp[:].indirect(T.repo[:, 16:40]), CP))]
+    parts = slice(0, 192), slice(192, 384)
+    for i, c in enumerate(parts):
+        v("scan", T.rp[:, c], T.hold32[:, c], T.d1[:, c], 0.0, A.mult, A.add, deps=("v",) if i == 0 else (), sem=two["scan"][i])
+    for i, c in enumerate(parts):
+        v("tr", T.sc2[:, c], T.rp[:, c], deps=(two["scan"][i],))
+    v("tr", T.sc2[:, 384:640], T.rp[:, 384:640], deps=(s_rp[0],))
+    x_s2 = v("tr", T.sc2[:, 640:1024], T.rp[:, 640:1024], deps=(s_rp[1],), cross=True)
+
+    wait("v", ("v", x_s2))
+    x_s3 = v("copy", T.gv[:, 0:256], T.sc2[:].indirect(T.off2[:, 0:16]), deps=(), cross=True)
+    s_g2 = op("s", "act", (T.gv[:, 256:512], T.sc2[:].indirect(T.off2[:, 16:32]), CP), (x_s2,))
+    x_st = choose(512, (x_s3, s_g2), T.key2, T.st)
+    for i, c in enumerate(halves):
+        v("ts", T.zi2[:, c], T.st[:, 256 * i + 3:256 * i + 256:4], TOP, None, A.mult, deps=(x_st[i],), sem=two["whole"][i])
+    s_zr = op("s", "act", (T.zrow[0:1, :], T.st[0:1, 3:512:4], CP), x_st)
+    b_z = op("g", "bc", (T.zb2[:], T.zi2[0:1, :], 128), two["whole"])
+    b_zf = op("g", "bc", (T.zf2[:], T.zrow[0:1, :], 128), (s_zr,))
+    for i, c in enumerate(halves):
+        v("ts", T.am[:, c], T.zi2[:, c], 896, None, A.bitwise_and, deps=(two["whole"][i],), sem=two["rank"][i])
+    for i, c in enumerate(halves):
+        v("ts", T.mb[:, 64 * i + 1:64 * i + 65], T.am[:, c], float(128 * me), None, A.is_equal, deps=(two["rank"][i],))
+    v("scan", T.ce[:], T.ones[:], T.mb[:, 0:128], 0.0, A.mult, A.add)
+    v("ts", T.pp[:], T.ce[:], T.ip[:], None, A.is_le)
+    v("scan", T.ks[:], T.pp[:], T.st[:, 3:512:4], 0.0, A.max, A.min)
+    v("ts", T.lr[:], T.mask16[:, 0:32], T.ks[:, 127:128], None, A.mult)
+    x_sj = v("ts", T.sj[:], T.zb2[:], 7, 7, A.logical_shift_right, A.bitwise_and, deps=(b_z,), cross=True)
+    v("tr", T.lt[:], T.lr[:])
+    x_mk = v("ts", T.mk[:], T.sj[:], T.spart[:], None, A.is_equal, deps=(x_sj,), cross=True)
+    x_ls, x_r8, s_r8 = fresh(), fresh(), fresh()
+    for a in range(4):
+        qa = slice(32 * a, 32 * a + 32)
+        v("scan", T.ls[qa, qa], T.hold16[qa, 0:32], T.lt[qa, :], 0.0, A.mult, A.add, deps=("v",) if a == 0 else (), sem=x_ls)
+    x_cum = v("scan", T.cum[:], T.ones[:], T.mk[:], 0.0, A.mult, A.add, deps=(x_mk,), cross=True)
+    for a, b in ((0, 1), (1, 0), (2, 3), (3, 2)):
+        out, src = [T.ls[32 * c:32 * c + 32, 32 * a + 15:32 * a + 32:16] for c in (b, a)]
+        if a < 2:
+            v("copy", out, src, deps=(x_ls,), sem=x_r8)
+        else:
+            op("s", "act", (out, src, CP), (x_ls,), sem=s_r8)
+    s_r9 = op("s", "act", (T.ls[64:128, 15:64:16], T.ls[0:64, 15:64:16], CP), (x_r8,))
+    v("copy", T.ls[0:64, 79:128:16], T.ls[64:128, 79:128:16], deps=(s_r8,))
+    s_mk = op("s", "act", (T.dup2[:], T.mk[:].indirect(T.dupo[:]), CP), (x_mk,))
+    x_cs = v("scan", T.cs[:], T.mask16[:], T.zf2[:], 0.0, A.max, A.min, deps=(b_zf,), cross=True)
+    v("ts", T.r8i[:], T.ls[:, 15:128:16], TOP, None, A.mult, deps=("v", x_r8, s_r8, s_r9))
+    v("ts", T.r8n[:], T.r8i[:], 127, None, A.bitwise_and)
+    x_i0 = v("ts", i8(0), T.cs[:, 15:128:16], TOP, None, A.mult, deps=(x_cs,), cross=True)
+    x_of = v("copy", T.offp[:], T.r8n[:], cross=True)
+    x_i2 = v("ts", i8(2), i8(0), 1023, None, A.bitwise_and, deps=(x_i0,), cross=True)
+    s_pk = op("s", "act", (T.pks[:], T.h1s[:].indirect(T.offp[:]), CP), (x_of, x_h1))
+    x_pk = v("copy", T.pk[:].bitcast(dt.uint32), T.h1q[:].bitcast(dt.uint32).indirect(T.offp[:]), deps=(x_of, x_h1), cross=True)
+
+    runs = [slice(16 * min(share), 16 * max(share) + 16) for share in PICKS_H]
+    send(near(T, topo, core, me, "kc", lambda i: T.pk[:, runs[i]].bitcast(dt.uint8)), (x_pk,))
+    send(near(T, topo, core, me, "ks", lambda i: T.pks[:, runs[i]]), (s_pk,))
+    for sem, src, dst in pick_calls(T, me):
+        send(far(T, topo, core, me, PICKS, "a2", src, dst), ())
+
+    base = float(128 - 128 * me)
+    v("tt", T.v2[:], T.cum[:].indirect(T.dupo[:]), T.dup2[:], A.mult, deps=(x_cum, s_mk))
+    v("ts", f8(4), i8(2), base, None, A.add, deps=(x_i2,))
+    x_i3 = v("ts", i8(3), i8(2), 7, None, A.logical_shift_right, deps=(), cross=True)
+    v("tr", T.vt[:], T.v2[:])
+    v("tt", f8(5), etab2, i8(2), A.subtract, deps=())
+    v("ts", f8(6), i8(3), 16.0, -1.0, A.mult, A.add, deps=(x_i3,))
+    v("scan", T.vs[:], T.hold32[:, 0:256], T.vt[:], 0.0, A.mult, A.add)
+    x_f7 = v("tt", f8(7), f8(6), f8(4), A.subtract, deps=(), cross=True)
+    v("ts", f8(8), cnt, 16.5, None, A.is_gt)
+    v("ts", f8(9), cnt, 0.5, None, A.is_gt, deps=())
+    v("tt", f8(10), f8(7), cnt, A.add, deps=(x_f7,))
+    v("tt", f8(12), f8(8), f8(5), A.mult)
+    v("tt", f8(11), f8(9), f8(8), A.subtract, deps=())
+    v("tt", f8(14), f8(12), f8(4), A.add)
+    v("tt", f8(13), f8(11), f8(10), A.mult, deps=())
+    v("tt", f8(15), f8(13), f8(14), A.add)
+    x_ix = v("copy", T.ixu[:], f8(15), cross=True)
+    v("tt", f8(16), f8(12), i8(2), A.add, deps=())
+    s_x2 = op("s", "act", (T.x2s[:], T.win2s[:].indirect(T.ixu[:]), CP), (x_ix, "a2"))
+    x_c2 = v("copy", T.cu2[:], f8(16), cross=True)
+    x_x2 = v("copy", T.x2[:].bitcast(dt.uint32), T.win2[:].bitcast(dt.uint32).indirect(T.ixu[:]), deps=(x_ix, "a2"), cross=True)
+    update(T.hs2, T.h2, T.x2, T.x2s, T.e2t, ld_e2, (x_x2, s_x2), x_a,
+           lambda: v("copy", T.base2[:], T.sc2[:].indirect(T.cu2[:]), deps=("v", x_c2)))
+    x_h2 = v("quant", T.h2q[:], T.h2s[:], T.h2[:], cross=True)
+    x_ch2 = v("copy", T.chr2[:], T.io1[:].indirect(T.cu2[:]), deps=(), cross=True)
+
+    m_y = op("t", "mm", (T.ps[:, 512:640], T.wq[:], T.ws[:], T.h2q[:], T.h2s[:], True, True), (x_h2, x_w))
+    m_g = op("t", "mm", (T.ps[:, 0:128], T.uq[:], T.us[:], T.h2q[:], T.h2s[:], True, True), (x_h2,))
+    dma("y", T.oc[:], T.h2q[:].bitcast(dt.uint8), (x_h2,))
+    for k in range(4):
+        dma("ys"[k // 2], T.osc[4 * k:4 * k + 4, :], T.h2s[32 * k:32 * k + 4, :], (x_h2,))
+    dma("y", T.ch[1:2, :], T.chr2[0:1, :], (x_ch2,))
+    s_y = op("s", "act", (T.yt[:], T.ps[:, 512:640], CP), (m_y,))
+    x_g = v("tt", T.gout[:], T.ps[:, 0:128], T.base2[:], A.add, deps=("v", m_g), cross=True)
+    dma("s", T.y[:], T.yt[:], (s_y,))
+    dma("y", T["g"][:], T.gout[0:1, :], (x_g,))
+
+    wait("v", ("v",))
+    for sem in sorted(total):
+        if sem != "v" and not any(seen.get((q, sem), 0) == total[sem] for q in Q):
+            wait("g", (sem,))

@@ -1,56 +1,44 @@
+import numpy as np
 from concourse.bass import DstId, RemoteDMATransfer
 from concourse.mybir import dt, AluOpType, ActivationFunctionType
 
 X4 = "float8_e4m3fn_x4"
 F, B, I, U16, U8 = "float32", "bfloat16", "int32", "uint16", "uint8"
-
-
-def _sb(n, d):
-    return ("sbuf", [128, n], d)
-
-
-SCRATCH = {
-    "e0t": _sb(512, B), "e1t": _sb(512, B), "e2t": _sb(512, B), "at": _sb(2048, B), "wt": _sb(512, B), "ut": _sb(4, B),
-    "ubig": _sb(512, B),
-    "pst": ("dram", [128, 4], I), "pl": ("dram", [8, 128, 4], I),
-    "l1": _sb(32, I), "lo": _sb(32, I), "l2": _sb(32, I),
-    "uq": _sb(128, X4), "us": _sb(128, U8), "aq": _sb(512, X4), "asc": _sb(512, U8), "wq": _sb(128, X4), "ws": _sb(128, U8),
-    "hall": _sb(1024, X4), "halls": _sb(1024, U8), "x1": _sb(128, X4), "x1s": _sb(128, U8),
-    "h1q": _sb(128, X4), "h1s": _sb(128, U8), "pk": _sb(128, X4), "pks": _sb(128, U8),
-    "win2": _sb(256, X4), "win2s": _sb(256, U8), "x2": _sb(128, X4), "x2s": _sb(128, U8),
-    "h2q": _sb(128, X4), "h2s": _sb(128, U8),
-    "ones": _sb(128, B), "hold32": _sb(512, B), "hold16": _sb(128, B), "rst": _sb(512, F), "pidx": _sb(1, I), "r15": _sb(1, I),
-    "r31": _sb(1, I), "ip": _sb(1, F), "sp31": _sb(1, F), "spx": _sb(1, F), "spart": _sb(1, F), "cmod": _sb(128, I),
-    "mask16": _sb(128, B), "ci": _sb(128, I), "repo": _sb(40, U16), "rsh": _sb(40, I), "dupo": _sb(16, U16),
-    "io1": _sb(1024, F), "eidx": _sb(512, F),
-    "off1": _sb(32, U16), "offo": _sb(32, U16), "offh": _sb(16, U16), "off2": _sb(32, U16), "er": _sb(512, F), "er2": _sb(512, F),
-    "kt": _sb(512, F), "kp": _sb(256, F), "key1": _sb(256, F), "key2": _sb(512, F), "st1": _sb(256, F),
-    "ew": _sb(128, F), "es": _sb(128, F), "ew2": _sb(128, F), "es2": _sb(128, F),
-    "sc": _sb(1024, F), "gv": _sb(512, F), "mx": _sb(512, F), "pm": _sb(512, B), "st": _sb(512, F),
-    "zb1": _sb(128, I), "zf1": _sb(128, F), "zi2": _sb(128, I), "zb2": _sb(128, I), "zrow": _sb(128, F), "zf2": _sb(128, F),
-    "sj": _sb(128, I), "mk": _sb(128, B), "th": _sb(128, B), "cum": _sb(128, B), "cs": _sb(128, F),
-    "dup1": _sb(256, B), "dup2": _sb(256, B), "v2": _sb(256, B), "vt": _sb(256, B), "vs": _sb(256, B),
-    "f8": _sb(160, F), "i8": _sb(32, I), "cu1": _sb(8, U16), "cu2": _sb(8, U16),
-    "base1": _sb(128, F), "bt": _sb(128, F), "gt": _sb(128, F), "sp": _sb(32, F), "d1": _sb(512, F), "rp": _sb(1024, F),
-    "sc2": _sb(1024, F), "base2": _sb(128, F), "gout": _sb(128, F), "yt": _sb(128, F),
-    "am": _sb(128, I), "mb": _sb(144, B), "ce": _sb(128, B), "pp": _sb(128, B), "ks": _sb(128, F), "lr": _sb(32, F),
-    "lt": _sb(32, F), "ls": _sb(128, F), "r8i": _sb(8, I), "r8n": _sb(8, I), "offp": _sb(8, U16),
-    "ixu": _sb(8, U16), "chr1": _sb(128, F), "chr2": _sb(128, F),
-    "hs1": _sb(512, F), "hs2": _sb(512, F), "h1": _sb(512, B), "h2": _sb(512, B),
-    "ps": ("psum", [128, 2048], F), "pr": ("psum", [128, 2048], F),
+SIZES = {
+    B: dict(e0t=512, e1t=512, e2t=512, at=2048, wt=512, ut=4, ubig=512, ones=128, hold32=256, hold16=128, rst=256, cb=144, mask16=128,
+            mneg=64, k2=128, pm=256, mk=256, cum=128, cum1=128, dup1=128, dup2=256, v1=128, vt1=128, vs1=128, v2=256,
+            vt=256, vs=256, pms=32, fl=128, mb=144, ce=256, lr=64, lt=64, ls=128, r8=8, h1=512, h2=512),
+    F: dict(pf=8, io1=1024, eidx=256, selr=96, selt=32, esm=24, er2=512, kp=256, key1=256, st1=256, ew2=192, es2=192, sc=1024, gv=256,
+            gw=512, mx=256, sel=24, cs=192, f8=160, base1=128, bt=128, gt=128, sp=32, d1=384, rp=1024, sc2=1024, base2=128,
+            gout=128, yt=128, lf=96, lt3=96, sf=224, k1r=128, k1=128, gT=512, mxs=40, kk=32, zt=160, zrow=128, zf2=128, ks=256,
+            chr1=128, chr2=128, hs1=512, rs=1024),
+    I: dict(l1=32, lo=32, l2=32, pi=8, ci=128, cmod=128, rsh=64, zi=128, zb2=128, sj=128, i8=48, si=96),
+    U16: dict(repo=64, dupo=16, selo=2, swo=6, rep1=8, offo=32, offh=16, cu1=8, cu2=8, off2=32, offp=8, ixu=8),
+    X4: dict(uq=128, aq=512, wq=128, hall=1024, x1=128, h1q=128, pk=128, win2=128, h2q=128),
+    U8: dict(us=128, asc=512, ws=128, halls=1024, x1s=128, h1s=128, pks=128, win2s=128, h2s=128),
 }
+SCRATCH = {name: ("sbuf", [128, n], d) for d, names in SIZES.items() for name, n in names.items()}
+SCRATCH.update({"pst": ("dram", [128, 4], I), "pl": ("dram", [8, 128, 4], I),
+                "ps": ("psum", [128, 2048], F), "pr": ("psum", [128, 2048], F)})
 
-REMOTE = ["al", "a0a", "a0b", "a0h", "ae", "a2", "left", "hl", "hc", "kc", "ks"]
-SEMAPHORES = REMOTE + ["v"] + ["s%d" % i for i in range(138)]
+REMOTE = ["al", "a0a", "a0b", "a0h", "a0i", "ae", "a2", "left", "hl", "hc", "kc", "ks"]
+SEMAPHORES = REMOTE + ["qv", "qs", "qt", "qg"] + ["d%d" % i for i in range(24)]
 A = AluOpType
-CP, IDN = ActivationFunctionType.Copy, ActivationFunctionType.Identity
+CP, IDN, ABS = ActivationFunctionType.Copy, ActivationFunctionType.Identity, ActivationFunctionType.Abs
 TOP = 2.0 ** 19
+LOW = -1.0e29
+BIG = 16384.0
+s_ = np.s_
 
-TIERS = (("a0a", {1: 2, 2: 2, 3: 2, 4: 2}), ("a0b", {5: 4, 6: 4}))
-TIER_H = ("a0h", {7: 8})
+TIERS = (("a0a", {1: 4, 2: 4}), ("a0b", {3: 4, 4: 4}))
+TIERS_H = (("a0h", {5: 4, 6: 4}), ("a0i", {7: 8}))
 LISTS = ({1: 2, 2: 2, 3: 2, 4: 2}, {5: 2, 6: 2, 7: 4})
 SCORES = {q: 1 for q in range(1, 8)}
-PICKS, PICKS_H = {1: 2, 2: 2, 3: 4}, ({4: 4, 5: 4}, {6: 4, 7: 4})
+PICKS = ({1: 2, 2: 2, 3: 4}, {3: 4, 1: 2, 2: 2})
+PICKS_H = ({4: 4, 5: 4}, {6: 4, 7: 4})
+
+WAIT, CYCLE, SLACK = 0.18, 0.001, 0.03
+LAG = {"a0a": 2.6, "a0h": 3.6, "a0i": 3.9, "a0b": 3.7, "al": 3.0, "ae": 1.6, "a2": 1.9}
 
 
 def helpers(core, topo):
@@ -104,12 +92,64 @@ def helper_program(g, core, T, topo, me, k):
     left = fused(g, T, topo, core, far(T, topo, core, me, LISTS[k], "al", lambda q: T.pst[:], lambda d: T.pl[(me - d) % N]))
     g.wait_ge(T.sem.hc, len(inner(T, topo, own, me)))
     piece = columns0(T, me)[k]
-    left += fused(g, T, topo, core, far(T, topo, core, me, TIER_H[1], TIER_H[0], lambda q: piece, lambda d: piece))
+    for sem, share in TIERS_H:
+        left += fused(g, T, topo, core, far(T, topo, core, me, share, sem, lambda q: piece, lambda d: piece))
     n = len(near(T, topo, own, me, "kc", lambda i: None)[k][1])
     for sem, src, dst in pick_calls(T, me):
         g.wait_ge(T.sem[sem], n)
         left += fused(g, T, topo, core, far(T, topo, core, me, PICKS_H[k], "a2", src, dst))
     g.wait_ge(T.sem.left, left)
+
+
+def place(view):
+    name, ix = view
+    where, shape, d = SCRATCH[name]
+    if where == "dram":
+        return name, 1, 1 << ix if isinstance(ix, int) else -1
+    p, c = range(*ix[0].indices(128)), range(*ix[1].indices(shape[1]))
+    if where == "psum":
+        return name, 1, 1 << c[0] // 512
+    return name, sum(1 << x for x in p), sum(1 << x for x in c)
+
+
+def width(view):
+    return len(range(*view[1][1].indices(SCRATCH[view[0]][1][1])))
+
+
+def order(steps):
+    n = len(steps)
+    after = [[] for s in steps]
+    for i, s in enumerate(steps):
+        for d in s["deps"] + s["behind"]:
+            after[d].append(i)
+    rest = [0.0] * n
+    for i in range(n - 1, -1, -1):
+        rest[i] = max([steps[i]["time"] + rest[j] if i in steps[j]["behind"] else steps[i]["lag"] + WAIT + rest[j] for j in after[i]]
+                      + [steps[i]["lag"]])
+    open_ = [len(s["deps"] + s["behind"]) for s in steps]
+    ready = [i for i in range(n) if not open_[i]]
+    end, free, out = [0.0] * n, {}, []
+    while ready:
+        start = {i: max([free.get(steps[i]["q"], 0.0)] + [end[d] + WAIT for d in steps[i]["deps"]]
+                        + [end[d] - steps[d]["lag"] + steps[d]["time"] for d in steps[i]["behind"]]) for i in ready}
+        pick = []
+        for q in {steps[i]["q"] for i in ready}:
+            mine = [i for i in ready if steps[i]["q"] == q]
+            while mine:
+                top = max(mine, key=lambda i: (rest[i], -i))
+                mine = [i for i in mine if start[i] < start[top] and start[i] + steps[i]["time"] <= start[top] + SLACK]
+            pick.append(top)
+        i = min(pick, key=lambda i: (start[i], i))
+        ready.remove(i)
+        out.append(i)
+        end[i] = start[i] + steps[i]["lag"]
+        if steps[i]["q"]:
+            free[steps[i]["q"]] = start[i] + steps[i]["time"]
+        for j in after[i]:
+            open_[j] -= 1
+            if not open_[j]:
+                ready.append(j)
+    return out
 
 
 def rank_program(g, core, T, topo):
@@ -121,333 +161,419 @@ def rank_program(g, core, T, topo):
         return
     N = len(T.cores)
     Q = {"g": g, "v": g.vector, "s": g.scalar, "t": g.tensor, "y": g.sync}
-    total, seen, used = {"left": 0}, {}, [0]
+    steps, seen_by = [], {}
 
-    def wait(q, deps):
-        for sem in deps:
-            assert sem != "v" or q == "v"
-            if seen.get((q, sem), 0) < total.get(sem, 0):
-                Q[q].wait_ge(T.sem[sem], total[sem])
-                seen[(q, sem)] = total[sem]
+    def add(q, call, reads, writes, time, lag=None, sem=None, count=1, deps=()):
+        deps = set(deps)
+        i = len(steps)
+        for views, wr in ((reads, False), (writes, True)):
+            for view in views:
+                if view[0] not in SCRATCH:
+                    continue
+                name, p, c = place(view)
+                w1 = wr or name in ("ps", "pr")
+                for j, w2, p2, c2 in seen_by.setdefault(name, []):
+                    if (w1 or w2) and p & p2 and c & c2 and j != i:
+                        deps.add(j)
+                seen_by[name].append((i, w1, p, c))
+        behind = [j for j in deps if steps[j]["sem"] == "left"] + [j for j in range(i) if q == steps[j]["q"] == "y"][-1:]
+        steps.append(dict(q=q, call=call, deps=sorted(deps - set(behind)), behind=behind, time=time, lag=time if lag is None else lag,
+                          sem=sem or "q" + q, count=count))
+        return i
 
-    def fresh():
-        used[0] += 1
-        return "s%d" % (used[0] - 1)
-
-    def mark(q, ins, n, cross, sem=None):
-        if sem is None:
-            sem = "v" if q == "v" and not cross else fresh()
-        total[sem] = total.get(sem, 0) + n
-        ins.then_inc(T.sem[sem], n)
-        return sem
-
-    def dma(q, out, in_, deps=(), sem=None):
-        wait(q, deps)
-        return mark(q, Q[q].dma_start(out, in_), 16, True, sem)
+    def ap(x, cast=None):
+        if not isinstance(x, tuple):
+            return x
+        a = T[x[0]][x[1]]
+        if cast is not None and SCRATCH.get(x[0], "...")[2] == X4:
+            a = a.bitcast(cast)
+        return a.indirect(ap(x[2])) if len(x) == 3 else a
 
     F_ = {"copy": g.vector.tensor_copy, "tt": g.vector.tensor_tensor, "ts": g.vector.tensor_scalar, "set": g.vector.memset,
           "scan": g.vector.tensor_tensor_scan, "tr": g.vector.transpose, "quant": g.vector.quantize_mx,
           "mm": g.tensor.matmul_mx, "act": g.scalar.activation, "iota": g.iota, "bc": g.partition_broadcast}
 
-    def op(q, name, args, deps=(), cross=True, sem=None, **kw):
-        wait(q, deps)
-        return mark(q, F_[name](*args, **kw), 1, cross, sem)
+    def op(name, *args, deps=(), **kw):
+        q = {"mm": "t", "act": "s", "iota": "g", "bc": "g"}.get(name, "v")
+        views = [a for a in args if isinstance(a, tuple)]
+        outs = 2 if name == "quant" else 1
+        reads = [a[:2] for a in views[outs:]] + [a[2] for a in views if len(a) == 3]
+        n = width(views[0])
+        if any(len(a) == 3 for a in views):
+            time = 0.065 + 1.5 * n * CYCLE
+        elif name in ("quant", "mm", "iota", "bc"):
+            time = {"quant": 0.15, "mm": 0.11, "iota": 0.16 + 2 * n * CYCLE, "bc": 0.17 + 4 * n * CYCLE}[name]
+        else:
+            short = all(SCRATCH[a[0]][2] in (B, U16) for a in views if width(a) == n) and name != "act"
+            both = name == "tt" and not any(a[0] in ("ps", "pr") for a in views)
+            time = max(64, n * (2 if both else 0.5 if short else 1)) * CYCLE + (0.03 if q == "s" else 0)
+        cast = dt.uint32 if name == "copy" else None
+        return add(q, lambda: F_[name](*[ap(a, cast) for a in args], **kw), reads, views[:outs], time, deps=deps)
 
-    def v(name, *args, deps=("v",), cross=False, sem=None):
-        return op("v", name, args, deps, cross, sem)
+    used = [0]
 
-    def send(parts, deps):
-        wait("g", deps)
-        total["left"] += fused(g, T, topo, core, parts)
+    def dma(q, out, in_, lag, deps=(), sem=None):
+        if sem is None:
+            used[0] += 1
+            sem = "d%d" % (used[0] - 1)
+        return add(q, lambda: Q[q].dma_start(ap(out, dt.uint8), ap(in_, dt.uint8)), [in_], [out], 0.05, lag, sem, 16, deps)
+
+    left = [0]
+
+    def send(parts, reads, deps=(), time=0.15):
+        left[0] += sum(len(p[1]) for p in parts)
+        return add("g", lambda: fused(g, T, topo, core, parts), reads, [], time, sem="left", count=0, deps=deps)
+
+    def arrive(sem, count, writes, sent):
+        return add(None, None, [], writes, 0.0, LAG[sem], sem, count, [sent])
 
     def count(*shares):
         return sum(n for share in shares for n in share.values())
 
-    total["al"], total["ae"], total["a2"] = count(*LISTS), count(SCORES), 2 * count(PICKS, *PICKS_H)
-    for sem, share in TIERS + (TIER_H,):
-        total[sem] = 2 * count(share)
-    arrivals = [sem for sem, share in TIERS + (TIER_H,)]
-    mine = slice(128 * me, 128 * me + 128)
+    def r(name, a=None, b=None, step=None, p=slice(None)):
+        return name, (p, slice(a, b, step))
+
+    def by(win, off):
+        return win + (off,)
+
+    def whole(name):
+        return name, s_[:]
+
+    def rank(name, s, n=128):
+        return r(name, n * s, n * s + n)
+
     halves = slice(0, 64), slice(64, 128)
-    two = {name: (fresh(), fresh()) for name in ("scan", "mark", "key", "whole", "rank")}
+    quarters = [slice(32 * a, 32 * a + 32) for a in range(4)]
+    io = "io1"
 
-    ld_e0 = dma("y", T.e0t[:], T.e0[:])
-    ld_ps = dma("s", T.pst[:], T.p2[:])
-    ld_u = dma("s", T.ut[:], T.u[:, 0:4])
-    ld_own = dma("s", T.pl[0], T.p2[:])
-    ld_l1, ld_lo = None, None
+    dma("y", r("e0t"), whole("e0"), 1.4)
+    dma("s", whole("pst"), whole("p2"), 1.0)
+    dma("s", r("ut"), ("u", s_[:, 0:4]), 1.5)
+    dma("s", ("pl", 0), whole("p2"), 1.5)
     for k in range(8):
-        ld_l1 = dma("y", T.l1[16 * k:16 * k + 16, :], T.p1[:], (), ld_l1)
+        dma("y", r("l1", p=slice(16 * k, 16 * k + 16)), whole("p1"), 1.3, sem="d20")
+    dma("y", r("at", 0, 512), ("a", s_[:, 0:512]), 1.9)
     for k in range(8):
-        ld_lo = dma("y", T.lo[16 * k:16 * k + 16, :], T.p2[:], (), ld_lo)
-    wait("y", arrivals[:1])
-    ld_a = dma("y", T.at[:], T.a[:])
-    wait("y", arrivals)
-    ld_e1 = dma("y", T.e1t[:], T.e1[:])
-    ld_l2 = dma("y", T.l2[:], T.pl[:], ("al", ld_own))
-    ld_w = dma("y", T.wt[:], T.w[:])
-    ld_e2 = dma("y", T.e2t[:], T.e2[:])
+        dma("y", r("lo", p=slice(16 * k, 16 * k + 16)), whole("p2"), 1.6, sem="d21")
 
-    i_p = op("g", "iota", (T.pidx[:], [[0, 1]], 0, 1))
-    i_0 = op("g", "iota", (T.io1[:, 0:128], [[1, 128]], 0, 0), allow_small_or_imprecise_dtypes=True)
-    i_1 = fresh()
+    pidx, r15, r31, rq = [r("pi", i, i + 1) for i in range(4)]
+    ip, sp31, spx, spart, pc, p16k, p4k, top0 = [r("pf", i, i + 1) for i in range(8)]
+    op("iota", pidx, [[0, 1]], 0, 1)
+    op("iota", r(io, 0, 128), [[1, 128]], 0, 0, allow_small_or_imprecise_dtypes=True)
     for k in range(1, 8):
-        op("s", "act", (T.io1[:, 128 * k:128 * k + 128], T.io1[:, 0:128], IDN), (i_0,), sem=i_1, bias=float(128 * k))
+        op("act", rank(io, k), r(io, 0, 128), IDN, bias=float(128 * k))
 
-    send(near(T, topo, core, me, "hl", lambda i: T.pst[:], 1), (ld_ps,))
-    x_h0 = v("quant", T.hall[:, mine], T.halls[:, mine], T.e0t[:], deps=(ld_e0,), cross=True)
-    for sem, share in TIERS:
-        if sem == TIERS[1][0]:
-            for c, piece in zip(helpers(core, topo), columns0(T, me)):
-                send([(c, inner(T, topo, core, me), "hc", piece, piece)], (x_h0,))
-        for piece in columns0(T, me):
-            send(far(T, topo, core, me, share, sem, lambda q: piece, lambda d: piece), (x_h0,))
+    sent = send(near(T, topo, core, me, "hl", lambda i: T.pst[:], 1), [whole("pst")], time=0.9)
+    arrive("al", count(*LISTS), [("pl", q) for q in range(1, N)], sent)
+    op("quant", rank("hall", me), rank("halls", me), r("e0t"))
+    for c, piece, name in zip(helpers(core, topo), columns0(T, me), ("hall", "halls")):
+        sent = send([(c, inner(T, topo, core, me), "hc", piece, piece)]
+                    + far(T, topo, core, me, TIERS[0][1], TIERS[0][0], lambda q: piece, lambda d: piece), [rank(name, me)], [sent])
+    first = sent
+    for piece in columns0(T, me):
+        sent = send(far(T, topo, core, me, TIERS[1][1], TIERS[1][0], lambda q: piece, lambda d: piece), [], [sent])
+    tiers = (TIERS[0], TIERS_H[0], TIERS_H[1], TIERS[1])
+    came = [arrive(sem, 2 * count(share), [rank(n, (me - q) % N) for q in share for n in ("hall", "halls")], first) for sem, share in tiers]
+    op("iota", r("selr", 0, 32), [[48, 2], [1, 8], [32, 2]], 0, 0, deps=[sent], allow_small_or_imprecise_dtypes=True)
+    op("iota", r("selr", 32, 96), [[16, 2], [0, 2], [1, 16]], 0, 0, deps=[sent], allow_small_or_imprecise_dtypes=True)
 
-    v("set", T.ones[:], 1.0)
-    v("ts", T.r15[:], T.pidx[:], 15, None, A.bitwise_and, deps=(i_p,))
-    v("ts", T.r31[:], T.pidx[:], 31, None, A.bitwise_and, deps=())
-    v("copy", T.ci[:], T.io1[:, 0:128], deps=(i_0,))
-    for buf, c in ((T.hold32[:, 0:256], 1.0), (T.hold16[:], 1.0), (T.rst[:, 0:256], 0.0), (T.pm[:, 0:512:4], 1.0), (T.mb[:, 0:1], 0.0)):
-        v("set", buf, c, deps=())
-    s_e = op("s", "act", (T.eidx[:], T.io1[:, 0:512], CP), (i_1,), scale=1024.0 / TOP)
+    dma("y", r("at", 512, 2048), ("a", s_[:, 512:2048]), 2.4, came[:1])
+    dma("y", r("l2"), whole("pl"), 1.4, came)
+    dma("y", r("e1t"), whole("e1"), 1.8)
+    dma("y", r("wt"), whole("w"), 2.2)
+    dma("y", r("e2t"), whole("e2"), 2.6)
+    dma("y", rank("win2", me, 16), r("hall", 128 * me, 128 * me + 16), 2.7, sem="d22")
+    dma("y", rank("win2s", me, 16), r("halls", 128 * me, 128 * me + 16), 2.7, sem="d22")
 
-    for a in range(2):
-        v("copy", T.offh[64 * a:64 * a + 64, :], T.l1[64 * a:64 * a + 64, 16 * a:16 * a + 16], deps=(ld_l1,))
-    v("copy", T.off1[:], T.l1[:], deps=())
+    rst3, hold4, dbl4, down = r("cb", 64, 80), r("cb", 80, 112), r("cb", 112, 144), r("ce", 128, 256)
+    for view, c in ((r("ones"), 1.0), (r("hold32"), 1.0), (r("hold16"), 1.0), (r("rst"), 0.0), (r("pm", 0, 256, 4), 1.0), (r("mb", 0, 1), BIG),
+                    (r("cb", 0, 80), 0.0), (hold4, 1.0), (dbl4, 2.0), (r("mxs"), LOW), (r("sel"), 0.0), (down, -BIG),
+                    (r("hold32", 0, 256, 32), 0.0), (r("hold16", 0, 128, 16), 0.0), (r("rst", 0, 256, 4), LOW), (r("cb", 0, 64, 16), -1024.0),
+                    (r("cb", 67, 80, 4), LOW), (r("cb", 80, 144, 4), 0.0), (r("zt", p=quarters[0]), 0.0)):
+        op("set", view, c)
+    op("ts", r15, pidx, 15, None, A.bitwise_and)
+    op("ts", r31, pidx, 31, None, A.bitwise_and)
+    op("ts", rq, pidx, 1, 16, A.logical_shift_right, A.bitwise_and)
+    op("copy", r("ci"), r(io, 0, 128))
+    op("act", r("eidx"), r(io, 0, 256), CP, scale=1024.0 / TOP)
+    op("act", r("d1"), r(io, 0, 384), CP, scale=0.0)
+    op("act", r("k2"), r(io, 0, 128), CP, scale=64.0)
+    op("copy", ip, r15)
+    op("copy", sp31, r31)
+    op("ts", r("cmod"), r("ci"), 15, None, A.bitwise_and)
+    op("ts", r("rsh"), r("ci", 0, 64), 1, None, A.logical_shift_right)
+    op("ts", pc, rq, ip, None, A.add)
+    op("ts", top0, ip, 0.5, BIG, A.add, A.mult)
+    op("ts", spx, sp31, float(me), 99.0, A.is_equal, A.mult)
+    op("ts", p16k, sp31, 16.0 * 1024.0 / TOP, None, A.mult)
+    op("ts", p4k, sp31, 256.0, None, A.mult)
+    op("ts", r("mask16"), r("cmod"), ip, None, A.is_equal)
+    op("ts", r("dupo"), r("rsh", 0, 16), 16.0, ip, A.mult, A.add)
+    op("copy", r("repo"), r("rsh"))
+    op("ts", r("swo", 0, 6, 5), r(io, 0, 32, 16), ip, None, A.add)
+    for c, b in ((1, 16.0), (3, 0.0)):
+        op("ts", r("swo", c, c + 2), r("ones", 0, 2), b, ip, A.mult, A.add)
+    for h in range(2):
+        op("copy", r("rep1", h, 8, 2), r(io, 16 * h + 3, 16 * h + 16, 4))
+        op("ts", r("esm", 16 + 4 * h, 20 + 4 * h), r(io, 0, 4), 64.0, p4k, A.mult, A.add)
+    op("tt", spart, spx, sp31, A.add)
+    op("ts", r("esm", 0, 16), r(io, 0, 16), 1024.0 / TOP, p16k, A.mult, A.add)
+    op("tr", r("selt"), r("selr", 0, 32))
+    op("ts", r("selo"), r(io, 0, 16, 8), r("selt", 0, 1), None, A.add)
+    op("ts", r("mneg"), r("selr", 32, 96), pc, -1024.0, A.not_equal, A.mult)
+
     for t in range(4):
-        v("ts", T.ubig[:, t:512:4], T.ones[:], T.ut[:, t:t + 1], None, A.mult, deps=("v", ld_u) if t == 0 else ())
-    x_off1 = v("copy", T.ip[:], T.r15[:], cross=True)
-    s_kp = op("s", "act", (T.kp[:], T.io1[:].indirect(T.offh[:]), CP), (x_off1, i_1), scale=1.0 / TOP)
-    s_er = op("s", "act", (T.er[:], T.io1[:].indirect(T.off1[:]), CP))
-    x_u = v("quant", T.uq[:], T.us[:], T.ubig[:], deps=("v",), cross=True)
-    v("set", T.hold32[:, 0:256:32], 0.0, deps=())
-    v("set", T.hold16[:, 0:128:16], 0.0, deps=())
-    v("set", T.rst[:, 0:256:4], -1.0e29, deps=())
-    v("copy", T.sp31[:], T.r31[:], deps=())
-    v("ts", T.cmod[:], T.ci[:], 15, None, A.bitwise_and, deps=())
-    v("ts", T.rsh[:], T.ci[:, 0:40], 1, None, A.logical_shift_right, deps=())
-    v("ts", T.spx[:], T.sp31[:], float(me), 99.0, A.is_equal, A.mult, deps=("v", x_off1))
-    v("ts", T.mask16[:], T.cmod[:], T.ip[:], None, A.is_equal, deps=())
-    v("ts", T.dupo[:], T.rsh[:, 0:16], 16.0, T.ip[:], A.mult, A.add, deps=())
-    x_rep = v("ts", T.repo[:], T.rsh[:], 12.0, None, A.add, deps=(), cross=True)
-    v("tt", T.spart[:], T.spx[:], T.sp31[:], A.add)
+        op("ts", r("ubig", t, 512, 4), r("ones"), r("ut", t, t + 1), None, A.mult)
+    op("quant", r("uq"), r("us"), r("ubig"))
     for a in range(2):
-        h = slice(64 * a, 64 * a + 64)
-        v("tt", T.key1[h, :], T.kp[h, :], T.eidx[h, 256 * a:256 * a + 256], A.add, deps=(s_kp, s_e))
-
-    def e0table(ew, es, row, deps):
-        v("tt", ew[:], row[:, 0:512:4], T.mask16[:], A.mult, deps=deps)
-        v("scan", es[:], T.hold16[:], ew[:], 0.0, A.mult, A.add)
-
-    x_offo = v("copy", T.offo[:], T.lo[:], deps=(ld_lo,), cross=True)
-    s_er2 = op("s", "act", (T.er2[:], T.io1[:].indirect(T.offo[:]), CP), (x_offo,))
-    e0table(T.ew, T.es, T.er, ("v", s_er))
-    v("set", T.d1[:], 0.0, deps=())
-    v("set", T.hold32[:, 256:512], 1.0, deps=())
-    v("set", T.rst[:, 256:512], 0.0, deps=())
-    v("set", T.hold32[:, 256:512:32], 0.0)
-    v("set", T.rst[:, 256:512:4], -1.0e29, deps=())
-    e0table(T.ew2, T.es2, T.er2, ("v", s_er2))
-
-    sc_done = []
-    order = [(me, x_h0)] + [((me - q) % N, sem) for sem, share in (TIERS[0], TIER_H, TIERS[1]) for q in share]
-    for i, (r, sem) in enumerate(order):
-        cs = slice(128 * r, 128 * r + 128)
-        bank = (T.ps if i < 4 else T.pr)[:, 512 * (i % 4):512 * (i % 4) + 128]
-        m = op("t", "mm", (bank, T.uq[:], T.us[:], T.hall[:, cs], T.halls[:, cs], True, True), (x_u, sem))
-        if i % 2:
-            sc_done.append(v("copy", T.sc[:, cs], bank, deps=(m,), cross=True))
-        else:
-            sc_done.append(op("s", "act", (T.sc[:, cs], bank, CP), (m,)))
-    arrived = [x_h0] + arrivals
-
-    def choose(w, parts, key, st):
-        h = w // 2
-        for i in range(2):
-            c = slice(h * i, h * i + h)
-            v("scan", T.mx[:, c], T.rst[:, c], T.gv[:, c], 0.0, A.add, A.max, deps=(parts[i],), sem=two["scan"][i])
-        for i in range(2):
-            for k in (1, 2, 3):
-                a, e = h * i + k, h * i + h
-                v("tt", T.pm[:, a:e:4], T.gv[:, a:e:4], T.mx[:, a - 1:e:4], A.is_gt, deps=(two["scan"][i],), sem=two["mark"][i])
-        for i in range(2):
-            c = slice(h * i, h * i + h)
-            v("scan", st[:, c], T.pm[:, c], key[:, c], 0.0, A.max, A.min, deps=(two["mark"][i],), sem=two["key"][i])
-        return two["key"]
+        op("copy", r("offh", p=halves[a]), r("l1", 16 * a, 16 * a + 16, p=halves[a]))
+    op("act", r("kp"), by(r(io), r("offh")), CP, scale=1.0 / TOP)
+    for a in range(2):
+        op("tt", rank("key1", a), rank("kp", a), rank("eidx", a), A.add)
+    op("copy", r("offo"), r("lo"))
+    for a in range(2):
+        op("act", rank("er2", a, 256), by(r(io), rank("offo", a, 16)), CP)
+    op("tt", r("ew2", 128, 192), r("kp", 0, 256, 4), r("mask16", 0, 64), A.mult)
+    op("scan", r("es2", 128, 192), r("hold16", 0, 64), r("ew2", 128, 192), 0.0, A.mult, A.add)
+    etab, etab2 = r("f8", 0, 4), r("es2", 15, 128, 16)
+    op("ts", etab, r("es2", 143, 192, 16), TOP, None, A.mult)
+    for a in range(2):
+        op("tt", rank("ew2", a, 64), r("er2", 256 * a, 256 * a + 256, 4), r("mask16", 0, 64), A.mult)
+    op("scan", r("es2", 0, 128), r("hold16"), r("ew2", 0, 128), 0.0, A.mult, A.add)
+    for i in range(4):
+        op("quant", rank("aq", i), rank("asc", i), rank("at", i, 512))
+    op("quant", r("wq"), r("ws"), r("wt"))
 
     def f8(i):
-        return T.f8[:, 8 * i:8 * i + 8]
+        return rank("f8", i, 8)
 
     def i8(i):
-        return T.i8[:, 8 * i:8 * i + 8]
+        return rank("i8", i, 8)
 
-    etab, etab2, cnt = T.es[:, 15:128:16], T.es2[:, 15:128:16], T.vs[:, 31:256:32]
+    def mm(out, w, x):
+        return op("mm", out, w[0], w[1], x[0], x[1], True, True)
 
-    def quant_a(i):
-        return v("quant", T.aq[:, 128 * i:128 * i + 128], T.asc[:, 128 * i:128 * i + 128], T.at[:, 512 * i:512 * i + 512], deps=(ld_a,),
-                 cross=True)
+    U = r("uq"), r("us")
 
-    def update(hs, h, X, Xs, e, ld_e, deps, x_a, between=None):
-        dep = []
-        for i in range(4):
-            s = slice(128 * i, 128 * i + 128)
-            m = op("t", "mm", (T.pr[:, 512 * i:512 * i + 128], T.aq[:, s], T.asc[:, s], X[:], Xs[:], True, True), tuple(deps) + (x_a[i],))
-            dep.append(op("s", "act", (hs[:, s], T.pr[:, 512 * i:512 * i + 128], CP), (m,), scale=0.05))
-        if between:
-            between()
-        for i in range(4):
-            v("tt", h[:, i:512:4], hs[:, 128 * i:128 * i + 128], e[:, i:512:4], A.add, deps=(dep[i], ld_e))
+    for i, s in enumerate([me] + [(me - q) % N for sem, share in tiers for q in share]):
+        bank = r("ps" if i < 4 else "pr", 512 * (i % 4), 512 * (i % 4) + 128)
+        mm(bank, U, (rank("hall", s), rank("halls", s)))
+        if i % 2:
+            op("copy", rank("sc", s), bank)
+        else:
+            op("act", rank("sc", s), bank, CP)
 
-    x_g1 = v("copy", T.gv[:, 0:128], T.sc[:].indirect(T.offh[:, 0:8]), deps=["v"] + sc_done, cross=True)
-    s_g1 = op("s", "act", (T.gv[:, 128:256], T.sc[:].indirect(T.offh[:, 8:16]), CP), sc_done)
-    x_st1 = choose(256, (x_g1, s_g1), T.key1, T.st1)
-    s_zf = fresh()
+    op("copy", rank("gv", 0), by(r("sc"), r("offh", 0, 8)))
+    op("act", rank("gv", 1), by(r("sc"), r("offh", 8, 16)), CP)
+    for i in range(2):
+        op("scan", rank("mx", i), rank("rst", i), rank("gv", i), 0.0, A.add, A.max)
+        for k in (1, 2, 3):
+            a, e = 128 * i + k, 128 * i + 128
+            op("tt", r("pm", a, e, 4), r("gv", a, e, 4), r("mx", a - 1, e, 4), A.is_gt)
+        op("scan", rank("st1", i), rank("pm", i), rank("key1", i), 0.0, A.max, A.min)
+
+    keys, chosen, th = r("st1", 3, 256, 4), r("i8", 36, 40), r("mk", 192, 256)
+    op("ts", r("zi", 0, 64), keys, TOP, None, A.mult)
+    op("ts", r("zi", 64, 128), r("zi", 0, 64), 7, 7, A.logical_shift_right, A.bitwise_and)
+    op("ts", th, r("zi", 64, 128), spart, 1.0e6, A.not_equal, A.mult)
+    op("ts", r("mk", 128, 192), r("zi", 64, 128), spart, None, A.is_equal)
+    op("act", r("dup1"), by(th, r("dupo", 0, 8)), CP)
+    for out in (r("cum1", 64, 128, p=halves[1]), r("cum1", 0, 64, p=halves[0])):
+        op("scan", out, r("ones", 0, 64, p=halves[0]), r("mk", 128, 192, p=halves[0]), -16.5, A.mult, A.add)
+    op("scan", r("cum1", 0, 64, p=halves[1]), r("ones", 0, 64, p=halves[1]), r("mk", 128, 192, p=halves[1]), r("cum1", 127, 128, p=halves[1]),
+       A.mult, A.add)
+    op("scan", r("cs", 128, 192), r("mask16", 0, 64), keys, 0.0, A.max, A.min)
+    op("ts", r("i8", 32, 36), r("cs", 143, 192, 16), TOP, None, A.mult)
+    op("ts", chosen, r("i8", 32, 36), 1023, None, A.bitwise_and)
+    op("copy", r("sel", 1, 9, 2), chosen)
+    op("tt", r("sel", 0, 8, 2), etab, chosen, A.subtract)
+    op("tt", r("v1"), by(r("cum1", 0, 64), r("dupo", 0, 8)), r("dup1"), A.is_gt)
+    op("tr", r("vt1"), r("v1"))
+    op("scan", r("vs1"), r("hold16"), r("vt1"), 0.0, A.mult, A.add)
+    op("scan", r("sel", 16, 24), r("vs1", 15, 128, 16), r("sel", 1, 9), r("sel", 0, 1), A.mult, A.add)
     for a, to in enumerate(halves):
         for there in halves:
-            v("ts", T.zb1[there, to], T.st1[to, 3:256:4], TOP, None, A.mult, deps=x_st1, sem=two["whole"][a])
-            op("s", "act", (T.zf1[there, to], T.st1[to, 3:256:4], CP), x_st1, sem=s_zf)
+            op("copy", r("cu1", 4 * a, 4 * a + 4, p=there), r("sel", 16, 24, 2, p=to))
+    op("act", r("x1s"), by(r("halls"), r("cu1")), CP)
+    op("copy", r("x1"), by(r("hall"), r("cu1")))
 
-    for i, c in enumerate(halves):
-        v("ts", T.sj[:, c], T.zb1[:, c], 7, 7, A.logical_shift_right, A.bitwise_and, deps=(two["whole"][i],), sem=two["rank"][i])
-    x_th = fresh()
-    for i, c in enumerate(halves):
-        v("ts", T.th[:, c], T.sj[:, c], T.spart[:], 1.0e6, A.not_equal, A.mult, deps=(two["rank"][i],), sem=x_th)
-    s_th = op("s", "act", (T.dup1[:], T.th[:].indirect(T.dupo[:]), CP), (x_th,))
-    v("ts", T.mk[:], T.sj[:], T.spart[:], None, A.is_equal, deps=())
-    x_cum1 = v("scan", T.cum[:], T.ones[:], T.mk[:], -16.5, A.mult, A.add, cross=True)
-    x_cs1 = v("scan", T.cs[:], T.mask16[:], T.zf1[:], 0.0, A.max, A.min, deps=(s_zf,), cross=True)
-    x_a = [quant_a(0)]
-    x_v1 = v("tt", T.v2[:], T.cum[:].indirect(T.dupo[:]), T.dup1[:], A.is_gt, deps=(x_cum1, s_th), cross=True)
-    x_i0 = v("ts", i8(0), T.cs[:, 15:128:16], TOP, None, A.mult, deps=(x_cs1,), cross=True)
-    x_vt = v("tr", T.vt[:], T.v2[:], deps=(x_v1,), cross=True)
-    x_i1 = v("ts", i8(1), i8(0), 1023, None, A.bitwise_and, deps=(x_i0,), cross=True)
-    v("scan", T.vs[:], T.hold32[:, 0:256], T.vt[:], 0.0, A.mult, A.add, deps=(x_vt,))
-    v("tt", f8(0), etab, i8(1), A.subtract, deps=(x_i1,))
-    v("tt", f8(1), cnt, f8(0), A.mult)
-    v("tt", f8(2), f8(1), i8(1), A.add)
-    x_c1 = v("copy", T.cu1[:], f8(2), cross=True)
+    def products(out, X):
+        for i in range(4):
+            mm(r("pr", 512 * i, 512 * i + 128), (rank("aq", i), rank("asc", i)), X)
+            op("act", out(i), r("pr", 512 * i, 512 * i + 128), CP, scale=0.05)
 
-    s_x1 = op("s", "act", (T.x1s[:], T.halls[:].indirect(T.cu1[:]), CP), [x_c1] + arrived)
-    s_b1 = op("s", "act", (T.base1[:], T.sc[:].indirect(T.cu1[:]), CP))
-    x_x1 = v("copy", T.x1[:].bitcast(dt.uint32), T.hall[:].bitcast(dt.uint32).indirect(T.cu1[:]), deps=[x_c1] + arrived, cross=True)
-    x_a += [quant_a(i) for i in (1, 2, 3)]
-    update(T.hs1, T.h1, T.x1, T.x1s, T.e1t, ld_e1, (x_x1, s_x1), x_a)
-    x_h1 = v("quant", T.h1q[:], T.h1s[:], T.h1[:], cross=True)
+    products(lambda i: rank("hs1", i), (r("x1"), r("x1s")))
+    op("act", r("base1"), by(r("sc"), r("cu1")), CP)
+    for i in range(4):
+        op("tt", r("h1", i, 512, 4), rank("hs1", i), r("e1t", i, 512, 4), A.add)
+    H1 = r("h1q"), r("h1s")
+    op("quant", H1[0], H1[1], r("h1"))
 
-    m = op("t", "mm", (T.ps[:, 0:128], T.uq[:], T.us[:], T.h1q[:], T.h1s[:], True, True), (x_h1,))
-    x_off2 = v("copy", T.off2[:], T.l2[:], deps=(ld_l2,), cross=True)
-    s_kt = op("s", "act", (T.kt[:], T.io1[:].indirect(T.off2[:]), CP), (x_off2,), scale=1.0 / TOP)
-    v("tr", T.bt[:], T.base1[:], deps=(s_b1,))
-    v("tr", T.gt[:], T.ps[:, 0:128], deps=(m,))
-    x_sp = v("tt", T.sp[:, 4 * me:4 * me + 4], T.gt[:, 0:128:32], T.bt[:, 0:128:32], A.add, cross=True)
+    mm(r("ps", 0, 128), U, H1)
+    op("tr", r("bt"), r("base1"))
+    op("tr", r("gt"), r("ps", 0, 128))
+    op("tt", rank("sp", me, 4), r("gt", 0, 128, 32), r("bt", 0, 128, 32), A.add)
     own_sp = T.sp[:, 4 * me:4 * me + 4]
-    send(far(T, topo, core, me, SCORES, "ae", lambda q: own_sp, lambda d: own_sp), (x_sp,))
+    sent = send(far(T, topo, core, me, SCORES, "ae", lambda q: own_sp, lambda d: own_sp), [rank("sp", me, 4)])
+    arrive("ae", count(SCORES), [rank("sp", s, 4) for s in range(N) if s != me], sent)
+    op("tt", rank("sc2", me), r("ps", 0, 128), r("base1"), A.add)
+    products(lambda i: rank("rs", 2 * i + 1), H1)
+    op("act", r("chr1"), by(r(io), r("cu1")), CP)
+    dma("y", ("ch", s_[0:1, :]), r("chr1", p=slice(0, 1)), 1.2, [sent], "d23")
 
-    v("quant", T.win2[:, 128:256], T.win2s[:, 128:256], T.h1[:], deps=())
-    x_w = v("quant", T.wq[:], T.ws[:], T.wt[:], deps=(ld_w,), cross=True)
-    v("tt", T.key2[:], T.kt[:], T.eidx[:], A.add, deps=(s_kt, s_e))
-    x_ch1 = v("copy", T.chr1[:], T.io1[:].indirect(T.cu1[:]), deps=(x_c1, i_1), cross=True)
-    dma("y", T.ch[0:1, :], T.chr1[0:1, :], (x_ch1,))
+    def sf(i):
+        return rank("sf", i, 32)
 
-    v("copy", T.d1[:, 0:384:32], T.sp[:, 0:12], deps=("v", "ae", x_sp))
-    s_rp = [op("s", "act", (T.rp[:, 384:640], T.sp[:].indirect(T.repo[:, 0:16]), CP), ("ae", x_sp, x_rep)),
-            op("s", "act", (T.rp[:, 640:1024], T.sp[:].indirect(T.repo[:, 16:40]), CP))]
-    parts = slice(0, 192), slice(192, 384)
-    for i, c in enumerate(parts):
-        v("scan", T.rp[:, c], T.hold32[:, c], T.d1[:, c], 0.0, A.mult, A.add, deps=("v",) if i == 0 else (), sem=two["scan"][i])
-    for i, c in enumerate(parts):
-        v("tr", T.sc2[:, c], T.rp[:, c], deps=(two["scan"][i],))
-    v("tr", T.sc2[:, 384:640], T.rp[:, 384:640], deps=(s_rp[0],))
-    x_s2 = v("tr", T.sc2[:, 640:1024], T.rp[:, 640:1024], deps=(s_rp[1],), cross=True)
+    def si(i):
+        return rank("si", i, 32)
 
-    wait("v", ("v", x_s2))
-    x_s3 = v("copy", T.gv[:, 0:256], T.sc2[:].indirect(T.off2[:, 0:16]), deps=(), cross=True)
-    s_g2 = op("s", "act", (T.gv[:, 256:512], T.sc2[:].indirect(T.off2[:, 16:32]), CP), (x_s2,))
-    x_st = choose(512, (x_s3, s_g2), T.key2, T.st)
-    for i, c in enumerate(halves):
-        v("ts", T.zi2[:, c], T.st[:, 256 * i + 3:256 * i + 256:4], TOP, None, A.mult, deps=(x_st[i],), sem=two["whole"][i])
-    s_zr = op("s", "act", (T.zrow[0:1, :], T.st[0:1, 3:512:4], CP), x_st)
-    b_z = op("g", "bc", (T.zb2[:], T.zi2[0:1, :], 128), two["whole"])
-    b_zf = op("g", "bc", (T.zf2[:], T.zrow[0:1, :], 128), (s_zr,))
-    for i, c in enumerate(halves):
-        v("ts", T.am[:, c], T.zi2[:, c], 896, None, A.bitwise_and, deps=(two["whole"][i],), sem=two["rank"][i])
-    for i, c in enumerate(halves):
-        v("ts", T.mb[:, 64 * i + 1:64 * i + 65], T.am[:, c], float(128 * me), None, A.is_equal, deps=(two["rank"][i],))
-    v("scan", T.ce[:], T.ones[:], T.mb[:, 0:128], 0.0, A.mult, A.add)
-    v("ts", T.pp[:], T.ce[:], T.ip[:], None, A.is_le)
-    v("scan", T.ks[:], T.pp[:], T.st[:, 3:512:4], 0.0, A.max, A.min)
-    v("ts", T.lr[:], T.mask16[:, 0:32], T.ks[:, 127:128], None, A.mult)
-    x_sj = v("ts", T.sj[:], T.zb2[:], 7, 7, A.logical_shift_right, A.bitwise_and, deps=(b_z,), cross=True)
-    v("tr", T.lt[:], T.lr[:])
-    x_mk = v("ts", T.mk[:], T.sj[:], T.spart[:], None, A.is_equal, deps=(x_sj,), cross=True)
-    x_ls, x_r8, s_r8 = fresh(), fresh(), fresh()
+    op("copy", r("lf"), by(r("l2"), r("swo")))
+    op("tr", r("lt3"), r("lf"))
+    op("copy", si(0), r("lt3", 0, 32))
+    op("copy", r("off2"), by(r("lt3"), r("selo")))
+    op("ts", si(1), si(0), 7, None, A.logical_shift_right)
+    op("ts", si(2), si(0), 127, None, A.bitwise_and)
+    op("ts", r("sf", 128, 144), r("lt3", 0, 16), 1.0 / TOP, None, A.mult)
+    op("ts", sf(0), si(1), float(me), 0.5, A.is_equal, A.mult)
+    op("tt", r("sf", 160, 176), r("sf", 128, 144), r("esm", 0, 16), A.add)
+    op("tt", sf(2), si(2), sf(0), A.mult)
+    op("scan", sf(1), dbl4, sf(0), 0.0, A.mult, A.add)
+    op("scan", sf(3), hold4, sf(2), 0.0, A.mult, A.add)
+    op("tt", r("sf", 99, 128, 4), r("sf", 99, 128, 4), r("esm", 16, 24), A.add)
+    op("act", r("k1r"), by(sf(3), r("rep1")), CP)
     for a in range(4):
-        qa = slice(32 * a, 32 * a + 32)
-        v("scan", T.ls[qa, qa], T.hold16[qa, 0:32], T.lt[qa, :], 0.0, A.mult, A.add, deps=("v",) if a == 0 else (), sem=x_ls)
-    x_cum = v("scan", T.cum[:], T.ones[:], T.mk[:], 0.0, A.mult, A.add, deps=(x_mk,), cross=True)
-    for a, b in ((0, 1), (1, 0), (2, 3), (3, 2)):
-        out, src = [T.ls[32 * c:32 * c + 32, 32 * a + 15:32 * a + 32:16] for c in (b, a)]
-        if a < 2:
-            v("copy", out, src, deps=(x_ls,), sem=x_r8)
+        op("tr", r("k1", a, 128, 4), rank("k1r", a, 32))
+
+    cut = [q for q in (1, 2, 3) if q == 1 or (me + q) % N == 0] + [4]
+    for a, b in zip(cut, cut[1:]):
+        op("copy", r("d1", 128 * a - 128, 128 * b - 128, 32), r("sp", 4 * ((me + a) % N), 4 * ((me + a) % N + b - a)))
+    for q in range(1, N):
+        s = (me + q) % N
+        if q < 4:
+            op("scan", rank("rp", s), r("hold32", 0, 128), rank("d1", q - 1), 0.0, A.mult, A.add)
         else:
-            op("s", "act", (out, src, CP), (x_ls,), sem=s_r8)
-    s_r9 = op("s", "act", (T.ls[64:128, 15:64:16], T.ls[0:64, 15:64:16], CP), (x_r8,))
-    v("copy", T.ls[0:64, 79:128:16], T.ls[64:128, 79:128:16], deps=(s_r8,))
-    s_mk = op("s", "act", (T.dup2[:], T.mk[:].indirect(T.dupo[:]), CP), (x_mk,))
-    x_cs = v("scan", T.cs[:], T.mask16[:], T.zf2[:], 0.0, A.max, A.min, deps=(b_zf,), cross=True)
-    v("ts", T.r8i[:], T.ls[:, 15:128:16], TOP, None, A.mult, deps=("v", x_r8, s_r8, s_r9))
-    v("ts", T.r8n[:], T.r8i[:], 127, None, A.bitwise_and)
-    x_i0 = v("ts", i8(0), T.cs[:, 15:128:16], TOP, None, A.mult, deps=(x_cs,), cross=True)
-    x_of = v("copy", T.offp[:], T.r8n[:], cross=True)
-    x_i2 = v("ts", i8(2), i8(0), 1023, None, A.bitwise_and, deps=(x_i0,), cross=True)
-    s_pk = op("s", "act", (T.pks[:], T.h1s[:].indirect(T.offp[:]), CP), (x_of, x_h1))
-    x_pk = v("copy", T.pk[:].bitcast(dt.uint32), T.h1q[:].bitcast(dt.uint32).indirect(T.offp[:]), deps=(x_of, x_h1), cross=True)
+            op("act", rank("rp", s), by(r("sp"), rank("repo", s, 8)), CP)
+        op("tr", rank("sc2", s), rank("rp", s))
 
-    runs = [slice(16 * min(share), 16 * max(share) + 16) for share in PICKS_H]
-    send(near(T, topo, core, me, "kc", lambda i: T.pk[:, runs[i]].bitcast(dt.uint8)), (x_pk,))
-    send(near(T, topo, core, me, "ks", lambda i: T.pks[:, runs[i]]), (s_pk,))
-    for sem, src, dst in pick_calls(T, me):
-        send(far(T, topo, core, me, PICKS, "a2", src, dst), ())
+    for h in range(2):
+        op("copy", rank("gw", h), by(r("sc2"), rank("off2", h, 8)))
+        op("act", rank("gw", 2 + h), by(r("sc2"), rank("off2", 2 + h, 8)), CP)
+    for h in (0, 2, 1, 3):
+        op("tr", rank("gT", h), rank("gw", h))
+    for h in range(2):
+        op("scan", r("mxs", 17 * h + 1, 17 * h + 17), r("gT", 16 * h, 512, 32), rst3, LOW, A.max, A.add)
+        op("tt", rank("pms", h, 16), r("gT", 16 * h, 512, 32), r("mxs", 17 * h, 17 * h + 16), A.is_gt)
+        op("scan", rank("kk", h, 16), rank("pms", h, 16), r("sf", 32 + 16 * h, 48 + 16 * h), 0.0, A.max, A.min)
+    op("ts", r("fl", 0, 64), by(r("kk"), r("rep1", 0, 4)), 0.5, BIG, A.not_equal, A.mult)
+    op("act", r("fl", 64, 128), by(r("kk"), r("rep1", 4, 8)), ABS, bias=-BIG, scale=2.0 * BIG)
+    for a in range(4):
+        op("tr", r("mb", 1 + a, 129, 4), rank("fl", a, 32))
+    op("scan", r("ce", 0, 128), down, r("mb", 0, 128), top0, A.add, A.add)
+    op("scan", rank("ks", 0), r("ce", 0, 128), r("k1"), 0.0, A.max, A.min)
+    op("scan", rank("ks", 1), r("ce", 0, 128), r("k2"), 0.0, A.max, A.min)
+    op("ts", r("lr"), r("mneg"), r("ks", 127, 128), r("ks", 255, 256), A.add, A.subtract)
+    op("tr", r("lt"), r("lr"))
+    for there in halves:
+        for a, to in enumerate(halves):
+            op("scan", r("ls", 64 * a, 64 * a + 64, p=there), r("cb", 0, 64, p=to), r("lt", p=to), 0.0, A.add, A.max)
+    for a in range(4):
+        op("tt", r("r8", p=quarters[a]), r("ls", 15, 128, 16, quarters[a]), r("ls", 15, 128, 16, quarters[a ^ 1]), A.max)
+    op("ts", r("offp"), r("r8"), 2.0, None, A.mult)
+    op("act", r("pks"), by(H1[1], r("offp")), CP)
+    op("copy", r("pk"), by(H1[0], r("offp")))
 
-    base = float(128 - 128 * me)
-    v("tt", T.v2[:], T.cum[:].indirect(T.dupo[:]), T.dup2[:], A.mult, deps=(x_cum, s_mk))
-    v("ts", f8(4), i8(2), base, None, A.add, deps=(x_i2,))
-    x_i3 = v("ts", i8(3), i8(2), 7, None, A.logical_shift_right, deps=(), cross=True)
-    v("tr", T.vt[:], T.v2[:])
-    v("tt", f8(5), etab2, i8(2), A.subtract, deps=())
-    v("ts", f8(6), i8(3), 16.0, -1.0, A.mult, A.add, deps=(x_i3,))
-    v("scan", T.vs[:], T.hold32[:, 0:256], T.vt[:], 0.0, A.mult, A.add)
-    x_f7 = v("tt", f8(7), f8(6), f8(4), A.subtract, deps=(), cross=True)
-    v("ts", f8(8), cnt, 16.5, None, A.is_gt)
-    v("ts", f8(9), cnt, 0.5, None, A.is_gt, deps=())
-    v("tt", f8(10), f8(7), cnt, A.add, deps=(x_f7,))
-    v("tt", f8(12), f8(8), f8(5), A.mult)
-    v("tt", f8(11), f8(9), f8(8), A.subtract, deps=())
-    v("tt", f8(14), f8(12), f8(4), A.add)
-    v("tt", f8(13), f8(11), f8(10), A.mult, deps=())
-    v("tt", f8(15), f8(13), f8(14), A.add)
-    x_ix = v("copy", T.ixu[:], f8(15), cross=True)
-    v("tt", f8(16), f8(12), i8(2), A.add, deps=())
-    s_x2 = op("s", "act", (T.x2s[:], T.win2s[:].indirect(T.ixu[:]), CP), (x_ix, "a2"))
-    x_c2 = v("copy", T.cu2[:], f8(16), cross=True)
-    x_x2 = v("copy", T.x2[:].bitcast(dt.uint32), T.win2[:].bitcast(dt.uint32).indirect(T.ixu[:]), deps=(x_ix, "a2"), cross=True)
-    update(T.hs2, T.h2, T.x2, T.x2s, T.e2t, ld_e2, (x_x2, s_x2), x_a,
-           lambda: v("copy", T.base2[:], T.sc2[:].indirect(T.cu2[:]), deps=("v", x_c2)))
-    x_h2 = v("quant", T.h2q[:], T.h2s[:], T.h2[:], cross=True)
-    x_ch2 = v("copy", T.chr2[:], T.io1[:].indirect(T.cu2[:]), deps=(), cross=True)
+    spans = [slice(16 * min(share), 16 * max(share) + 16) for share in PICKS_H]
+    sent = send(near(T, topo, core, me, "kc", lambda i: T.pk[:, spans[i]].bitcast(dt.uint8)), [r("pk")])
+    first = sent = send(near(T, topo, core, me, "ks", lambda i: T.pks[:, spans[i]]), [r("pks")], [sent])
+    for share, (sem, src, dst) in zip(PICKS, pick_calls(T, me)):
+        sent = send(far(T, topo, core, me, share, "a2", src, dst), [], [sent])
+    arrive("a2", count(*PICKS) + 2 * count(*PICKS_H), [rank(n, s, 16) for s in range(N) if s != me for n in ("win2", "win2s")], first)
 
-    m_y = op("t", "mm", (T.ps[:, 512:640], T.wq[:], T.ws[:], T.h2q[:], T.h2s[:], True, True), (x_h2, x_w))
-    m_g = op("t", "mm", (T.ps[:, 0:128], T.uq[:], T.us[:], T.h2q[:], T.h2s[:], True, True), (x_h2,))
-    dma("y", T.oc[:], T.h2q[:].bitcast(dt.uint8), (x_h2,))
+    q0 = quarters[0]
+    op("scan", r("zt", 8, 136, 8, q0), r("pms", 0, 16, p=q0), r("sf", 160, 176, p=q0), 0.0, A.max, A.min)
+    for a in range(4):
+        op("tr", r("zrow", a, 128, 4, q0), r("zt", 32 * a + 32, 32 * a + 64, p=q0))
+    op("bc", r("zf2"), r("zrow", p=slice(0, 1)), 128)
+    cnt, mk = r("vs", 31, 256, 32), r("mk", 0, 128)
+    op("ts", r("zb2"), r("zf2"), TOP, None, A.mult)
+    op("scan", r("cs", 0, 128), r("mask16"), r("zf2"), 0.0, A.max, A.min)
+    op("ts", r("sj"), r("zb2"), 7, 7, A.logical_shift_right, A.bitwise_and)
+    op("ts", i8(0), r("cs", 15, 128, 16), TOP, None, A.mult)
+    op("ts", mk, r("sj"), spart, None, A.is_equal)
+    op("act", r("dup2"), by(mk, r("dupo")), CP)
+    op("ts", i8(2), i8(0), 1023, None, A.bitwise_and)
+    op("scan", r("cum"), r("ones"), mk, 0.0, A.mult, A.add)
+    op("ts", f8(4), i8(2), float(128 - 128 * me), None, A.add)
+    op("ts", i8(3), i8(2), 7, None, A.logical_shift_right)
+    op("tt", f8(5), etab2, i8(2), A.subtract)
+    for h in range(2):
+        op("tt", rank("v2", h), by(r("cum"), rank("dupo", h, 8)), rank("dup2", h), A.mult)
+    op("ts", f8(6), i8(3), 16.0, -1.0, A.mult, A.add)
+    op("tr", r("vt"), r("v2"))
+    op("tt", f8(7), f8(6), f8(4), A.subtract)
+    op("scan", r("vs"), r("hold32"), r("vt"), 0.0, A.mult, A.add)
+    op("ts", f8(8), cnt, 16.5, None, A.is_gt)
+    op("ts", f8(9), cnt, 0.5, None, A.is_gt)
+    op("tt", f8(10), f8(7), cnt, A.add)
+    op("tt", f8(12), f8(8), f8(5), A.mult)
+    op("tt", f8(11), f8(9), f8(8), A.subtract)
+    op("tt", f8(14), f8(12), f8(4), A.add)
+    op("tt", f8(13), f8(11), f8(10), A.mult)
+    op("tt", f8(16), f8(12), i8(2), A.add)
+    op("tt", f8(15), f8(13), f8(14), A.add)
+    op("copy", r("cu2"), f8(16))
+    op("copy", r("ixu"), f8(15))
+    op("act", r("base2"), by(r("sc2"), r("cu2")), CP)
+    op("act", r("chr2"), by(r(io), r("cu2")), CP)
+    dma("y", ("ch", s_[1:2, :]), r("chr2", p=slice(0, 1)), 1.2, sem="d23")
+
+    products(lambda i: rank("rs", 2 * i), (r("win2"), r("win2s")))
+    for i in range(4):
+        op("tt", r("h2", i, 512, 4), by(rank("rs", i, 256), r("ixu")), r("e2t", i, 512, 4), A.add)
+    H2 = r("h2q"), r("h2s")
+    op("quant", H2[0], H2[1], r("h2"))
+
+    mm(r("ps", 512, 640), (r("wq"), r("ws")), H2)
+    mm(r("ps", 0, 128), U, H2)
+    dma("y", whole("oc"), H2[0], 1.4, sem="d23")
     for k in range(4):
-        dma("ys"[k // 2], T.osc[4 * k:4 * k + 4, :], T.h2s[32 * k:32 * k + 4, :], (x_h2,))
-    dma("y", T.ch[1:2, :], T.chr2[0:1, :], (x_ch2,))
-    s_y = op("s", "act", (T.yt[:], T.ps[:, 512:640], CP), (m_y,))
-    x_g = v("tt", T.gout[:], T.ps[:, 0:128], T.base2[:], A.add, deps=("v", m_g), cross=True)
-    dma("s", T.y[:], T.yt[:], (s_y,))
-    dma("y", T["g"][:], T.gout[0:1, :], (x_g,))
+        dma("ys"[k // 2], ("osc", s_[4 * k:4 * k + 4, :]), r("h2s", p=slice(32 * k, 32 * k + 4)), 1.2, sem="d23")
+    op("act", r("yt"), r("ps", 512, 640), CP)
+    op("tt", r("gout"), r("ps", 0, 128), r("base2"), A.add)
+    dma("s", whole("y"), r("yt"), 1.4, sem="d23")
+    dma("y", whole("g"), r("gout", p=slice(0, 1)), 1.2, sem="d23")
 
-    wait("v", ("v",))
+    seq = order(steps)
+    total, upto = {}, {}
+    for i in seq:
+        s = steps[i]
+        total[s["sem"]] = total.get(s["sem"], 0) + s["count"]
+        upto[i] = total[s["sem"]]
+    total["left"] = left[0]
+    known, done, waited = {q: 0 for q in Q}, {}, {}
+    before = {q: 0 for q in Q}
+    for i in seq:
+        s = steps[i]
+        q = s["q"]
+        if q is None:
+            done[i] = 1 << i
+            continue
+        for d in sorted(s["deps"], key=lambda d: -seq.index(d)):
+            t = steps[d]
+            if known[q] >> d & 1:
+                continue
+            n = upto[d] if t["sem"][0] == "q" else total[t["sem"]]
+            if waited.get((q, t["sem"]), 0) < n:
+                Q[q].wait_ge(T.sem[t["sem"]], n)
+                waited[q, t["sem"]] = n
+            known[q] |= done[d]
+        ins = s["call"]()
+        if s["count"]:
+            ins.then_inc(T.sem[s["sem"]], s["count"])
+        done[i] = known[q] | 1 << i
+        if s["sem"][0] == "q":
+            done[i] |= before[q]
+            before[q] = done[i]
     for sem in sorted(total):
-        if sem != "v" and not any(seen.get((q, sem), 0) == total[sem] for q in Q):
-            wait("g", (sem,))
+        if all(waited.get((q, sem), 0) < total[sem] for q in Q):
+            g.wait_ge(T.sem[sem], total[sem])

@@ -5,17 +5,16 @@ from concourse.mybir import dt, AluOpType, ActivationFunctionType
 X4 = "float8_e4m3fn_x4"
 F, B, I, U16, U8 = "float32", "bfloat16", "int32", "uint16", "uint8"
 SIZES = {
-    B: dict(e0t=512, e1t=512, e2t=512, at=2048, wt=512, ut=4, ubig=512, ones=128, hold32=256, hold16=128, rst=256, cb=144, mask16=128,
-            mneg=64, k2=128, pm=256, mk=256, cum=128, cum1=128, dup1=128, dup2=256, v1=128, vt1=128, vs1=128, v2=256,
-            vt=256, vs=256, pms=32, fl=128, mb=144, ce=256, lr=64, lt=64, ls=128, r8=8, h1=512, h2=512),
-    F: dict(pf=8, io1=1024, eidx=256, selr=96, selt=32, esm=24, er2=512, kp=256, key1=256, st1=256, ew2=192, es2=192, sc=1024, gv=256,
-            gw=512, mx=256, sel=24, cs=192, f8=160, base1=128, bt=128, gt=128, sp=32, d1=384, rp=1024, sc2=1024, base2=128,
-            gout=128, yt=128, lf=96, lt3=96, sf=224, k1r=128, k1=128, gT=512, mxs=40, kk=32, zt=160, zrow=128, zf2=128, ks=256,
-            chr1=128, chr2=128, hs1=512, rs=1024),
-    I: dict(l1=32, lo=32, l2=32, pi=8, ci=128, cmod=128, rsh=64, zi=128, zb2=128, sj=128, i8=48, si=96),
-    U16: dict(repo=64, dupo=16, selo=2, swo=6, rep1=8, offo=32, offh=16, cu1=8, cu2=8, off2=32, offp=8, ixu=8),
-    X4: dict(uq=128, aq=512, wq=128, hall=1024, x1=128, h1q=128, pk=128, win2=128, h2q=128),
-    U8: dict(us=128, asc=512, ws=128, halls=1024, x1s=128, h1s=128, pks=128, win2s=128, h2s=128),
+    B: dict(e0t=512, e1t=512, e2t=512, at=2048, wt=512, ut=4, ubig=512, ones=128, hold32=256, hold16=128, rst=256, cb=192, mask16=128,
+            mneg=64, k2=128, pm=256, wn=768, mk=192, cum=128, cum1=128, dup1=128, dup2=256, v1=128, vt1=128, vs1=256, v2=256,
+            vt=256, vs=256, pm2=512, hm2=512, cw2=512, won2=520, ce=128, hold8=128, lr=64, lt=64, ls=128, r8=8, h1=512, h2=512),
+    F: dict(pf=32, io1=1024, em=256, selr=64, er2=512, ce2=512, e2s=512, wcol=1024, col2=512, k1=512, mx2=512, kp=256, key1=256,
+            st1=256, ew2=128, es2=192, sc=1024, gv=256, gw=512, mx=256, sel=24, cs=192, f8=160, base1=128, bt=128, gt=128, sp=32,
+            d1=256, rp=1024, sc2=1024, base2=128, gout=128, yt=128, zf2=256, ks=256, chr=256, hs1=1024, rs=1024),
+    I: dict(l1=32, lo=32, l2=32, pi=8, ci=128, cmod=192, rsh=64, zi=16, zb2=128, sj=128, i8=32, si=32),
+    U16: dict(repo=64, dupo=24, offo=32, offh=32, cu1=32, cu2=8, off2=64, offp=8, ixu=8),
+    X4: dict(uq=128, aq=512, wq=128, hall=1024, x1=256, h1q=128, pk=128, win2=128, h2q=128),
+    U8: dict(us=128, asc=512, ws=128, halls=1024, x1s=256, h1s=128, pks=128, win2s=128, h2s=128),
 }
 SCRATCH = {name: ("sbuf", [128, n], d) for d, names in SIZES.items() for name, n in names.items()}
 SCRATCH.update({"pst": ("dram", [128, 4], I), "pl": ("dram", [8, 128, 4], I),
@@ -24,8 +23,7 @@ SCRATCH.update({"pst": ("dram", [128, 4], I), "pl": ("dram", [8, 128, 4], I),
 REMOTE = ["al", "a0a", "a0b", "a0h", "a0i", "ae", "a2", "left", "hl", "hc", "kc", "ks"]
 SEMAPHORES = REMOTE + ["qv", "qs", "qt", "qg"] + ["d%d" % i for i in range(24)]
 A = AluOpType
-CP, IDN, ABS = ActivationFunctionType.Copy, ActivationFunctionType.Identity, ActivationFunctionType.Abs
-TOP = 2.0 ** 19
+CP, IDN = ActivationFunctionType.Copy, ActivationFunctionType.Identity
 LOW = -1.0e29
 BIG = 16384.0
 s_ = np.s_
@@ -37,8 +35,10 @@ SCORES = {q: 1 for q in range(1, 8)}
 PICKS = ({1: 2, 2: 2, 3: 4}, {3: 4, 1: 2, 2: 2})
 PICKS_H = ({4: 4, 5: 4}, {6: 4, 7: 4})
 
-WAIT, CYCLE, SLACK = 0.18, 0.001, 0.03
-LAG = {"a0a": 2.6, "a0h": 3.6, "a0i": 3.9, "a0b": 3.7, "al": 3.0, "ae": 1.6, "a2": 1.9}
+WAIT, CYCLE, SLACK, TRIES = 0.18, 0.001, 0.03, 1200
+CASES = ((0.14, 1.0, 1.15), (0.2, 0.9, 1.05), (0.17, 1.0, 0.8), (0.16, 1.2, 1.0))
+LAG = {"a0a": 2.2, "a0h": 3.7, "a0i": 4.3, "a0b": 3.8, "al": 3.0, "ae": 1.8, "a2": 2.6}
+ORDER = []
 
 
 def helpers(core, topo):
@@ -118,38 +118,70 @@ def width(view):
 
 def order(steps):
     n = len(steps)
+    q, time, lag = [[s[k] for s in steps] for k in ("q", "time", "lag")]
+    deps, behind = [s["deps"] for s in steps], [s["behind"] for s in steps]
     after = [[] for s in steps]
-    for i, s in enumerate(steps):
-        for d in s["deps"] + s["behind"]:
+    for i in range(n):
+        for d in deps[i] + behind[i]:
             after[d].append(i)
     rest = [0.0] * n
     for i in range(n - 1, -1, -1):
-        rest[i] = max([steps[i]["time"] + rest[j] if i in steps[j]["behind"] else steps[i]["lag"] + WAIT + rest[j] for j in after[i]]
-                      + [steps[i]["lag"]])
-    open_ = [len(s["deps"] + s["behind"]) for s in steps]
-    ready = [i for i in range(n) if not open_[i]]
-    end, free, out = [0.0] * n, {}, []
-    while ready:
-        start = {i: max([free.get(steps[i]["q"], 0.0)] + [end[d] + WAIT for d in steps[i]["deps"]]
-                        + [end[d] - steps[d]["lag"] + steps[d]["time"] for d in steps[i]["behind"]]) for i in ready}
-        pick = []
-        for q in {steps[i]["q"] for i in ready}:
-            mine = [i for i in ready if steps[i]["q"] == q]
-            while mine:
-                top = max(mine, key=lambda i: (rest[i], -i))
-                mine = [i for i in mine if start[i] < start[top] and start[i] + steps[i]["time"] <= start[top] + SLACK]
-            pick.append(top)
-        i = min(pick, key=lambda i: (start[i], i))
-        ready.remove(i)
-        out.append(i)
-        end[i] = start[i] + steps[i]["lag"]
-        if steps[i]["q"]:
-            free[steps[i]["q"]] = start[i] + steps[i]["time"]
-        for j in after[i]:
-            open_[j] -= 1
-            if not open_[j]:
-                ready.append(j)
-    return out
+        rest[i] = max([time[i] + rest[j] if i in behind[j] else lag[i] + WAIT + rest[j] for j in after[i]] + [lag[i]])
+
+    def lay(way):
+        open_ = [len(deps[i]) + len(behind[i]) for i in range(n)]
+        ready, since, free, out = {}, [0.0] * n, {}, []
+        for i in range(n):
+            if not open_[i]:
+                ready.setdefault(q[i], []).append(i)
+        while len(out) < n:
+            best = None
+            for k, mine in ready.items():
+                f = free.get(k, 0.0)
+                while mine:
+                    top = max(mine, key=lambda i: way[i])
+                    t = max(f, since[top])
+                    mine = [i for i in mine if since[i] < t and f < t and max(f, since[i]) + time[i] <= t + SLACK]
+                    pick = t, top
+                if ready[k] and (best is None or pick < best):
+                    best = pick
+            t, i = best
+            ready[q[i]].remove(i)
+            out.append(i)
+            if q[i]:
+                free[q[i]] = t + time[i]
+            for j in after[i]:
+                since[j] = max(since[j], t + time[i] if i in behind[j] else t + lag[i] + WAIT)
+                open_[j] -= 1
+                if not open_[j]:
+                    ready.setdefault(q[j], []).append(j)
+        return out
+
+    def span(seq):
+        total = 0.0
+        for wait, work, away in CASES:
+            start, free = [0.0] * n, {}
+            took = [lag[i] * (work if lag[i] == time[i] else away) for i in range(n)]
+            for i in seq:
+                start[i] = max([free.get(q[i], 0.0)] + [start[d] + took[d] + wait for d in deps[i]] + [start[d] + time[d] for d in behind[i]])
+                if q[i]:
+                    free[q[i]] = start[i] + time[i] * work
+            total += max(start[i] + took[i] for i in range(n))
+        return total
+
+    rng = np.random.RandomState(0)
+    way = [x - 1e-6 * i for i, x in enumerate(rest)]
+    seq = lay(way)
+    least = span(seq)
+    for k in range(TRIES):
+        other = list(way)
+        for i in rng.randint(0, n, 1 + k % 12):
+            other[i] += float(rng.normal()) * 0.4
+        s = lay(other)
+        t = span(s)
+        if t < least:
+            way, seq, least = other, s, t
+    return seq
 
 
 def rank_program(g, core, T, topo):
@@ -163,7 +195,7 @@ def rank_program(g, core, T, topo):
     Q = {"g": g, "v": g.vector, "s": g.scalar, "t": g.tensor, "y": g.sync}
     steps, seen_by = [], {}
 
-    def add(q, call, reads, writes, time, lag=None, sem=None, count=1, deps=()):
+    def add(q, call, reads, writes, time, lag=None, sem=None, count=1, deps=(), behind=()):
         deps = set(deps)
         i = len(steps)
         for views, wr in ((reads, False), (writes, True)):
@@ -176,7 +208,7 @@ def rank_program(g, core, T, topo):
                     if (w1 or w2) and p & p2 and c & c2 and j != i:
                         deps.add(j)
                 seen_by[name].append((i, w1, p, c))
-        behind = [j for j in deps if steps[j]["sem"] == "left"] + [j for j in range(i) if q == steps[j]["q"] == "y"][-1:]
+        behind = list(behind) + [j for j in deps if steps[j]["sem"] == "left"] + [j for j in range(i) if q == steps[j]["q"] == "y"][-1:]
         steps.append(dict(q=q, call=call, deps=sorted(deps - set(behind)), behind=behind, time=time, lag=time if lag is None else lag,
                           sem=sem or "q" + q, count=count))
         return i
@@ -193,7 +225,7 @@ def rank_program(g, core, T, topo):
           "scan": g.vector.tensor_tensor_scan, "tr": g.vector.transpose, "quant": g.vector.quantize_mx,
           "mm": g.tensor.matmul_mx, "act": g.scalar.activation, "iota": g.iota, "bc": g.partition_broadcast}
 
-    def op(name, *args, deps=(), **kw):
+    def op(name, *args, deps=(), behind=(), **kw):
         q = {"mm": "t", "act": "s", "iota": "g", "bc": "g"}.get(name, "v")
         views = [a for a in args if isinstance(a, tuple)]
         outs = 2 if name == "quant" else 1
@@ -202,13 +234,13 @@ def rank_program(g, core, T, topo):
         if any(len(a) == 3 for a in views):
             time = 0.065 + 1.5 * n * CYCLE
         elif name in ("quant", "mm", "iota", "bc"):
-            time = {"quant": 0.15, "mm": 0.11, "iota": 0.16 + 2 * n * CYCLE, "bc": 0.17 + 4 * n * CYCLE}[name]
+            time = {"quant": 0.15, "mm": 0.13, "iota": 0.16 + 2 * n * CYCLE, "bc": 0.17 + 4 * n * CYCLE}[name]
         else:
             short = all(SCRATCH[a[0]][2] in (B, U16) for a in views if width(a) == n) and name != "act"
             both = name == "tt" and not any(a[0] in ("ps", "pr") for a in views)
             time = max(64, n * (2 if both else 0.5 if short else 1)) * CYCLE + (0.03 if q == "s" else 0)
         cast = dt.uint32 if name == "copy" else None
-        return add(q, lambda: F_[name](*[ap(a, cast) for a in args], **kw), reads, views[:outs], time, deps=deps)
+        return add(q, lambda: F_[name](*[ap(a, cast) for a in args], **kw), reads, views[:outs], time, deps=deps, behind=behind)
 
     used = [0]
 
@@ -252,12 +284,12 @@ def rank_program(g, core, T, topo):
     dma("s", ("pl", 0), whole("p2"), 1.5)
     for k in range(8):
         dma("y", r("l1", p=slice(16 * k, 16 * k + 16)), whole("p1"), 1.3, sem="d20")
-    dma("y", r("at", 0, 512), ("a", s_[:, 0:512]), 1.9)
+    dma("y", r("at", 0, 1024), ("a", s_[:, 0:1024]), 2.2)
     for k in range(8):
         dma("y", r("lo", p=slice(16 * k, 16 * k + 16)), whole("p2"), 1.6, sem="d21")
 
-    pidx, r15, r31, rq = [r("pi", i, i + 1) for i in range(4)]
-    ip, sp31, spx, spart, pc, p16k, p4k, top0 = [r("pf", i, i + 1) for i in range(8)]
+    pidx, r15, r31, rq, r64 = [r("pi", i, i + 1) for i in range(5)]
+    ip, sp31, spx, spart, pc, t8, t8x, top0, ph = [r("pf", i, i + 1) for i in range(9)]
     op("iota", pidx, [[0, 1]], 0, 1)
     op("iota", r(io, 0, 128), [[1, 128]], 0, 0, allow_small_or_imprecise_dtypes=True)
     for k in range(1, 8):
@@ -274,10 +306,9 @@ def rank_program(g, core, T, topo):
         sent = send(far(T, topo, core, me, TIERS[1][1], TIERS[1][0], lambda q: piece, lambda d: piece), [], [sent])
     tiers = (TIERS[0], TIERS_H[0], TIERS_H[1], TIERS[1])
     came = [arrive(sem, 2 * count(share), [rank(n, (me - q) % N) for q in share for n in ("hall", "halls")], first) for sem, share in tiers]
-    op("iota", r("selr", 0, 32), [[48, 2], [1, 8], [32, 2]], 0, 0, deps=[sent], allow_small_or_imprecise_dtypes=True)
-    op("iota", r("selr", 32, 96), [[16, 2], [0, 2], [1, 16]], 0, 0, deps=[sent], allow_small_or_imprecise_dtypes=True)
+    op("iota", r("selr"), [[16, 2], [0, 2], [1, 16]], 0, 0, deps=[sent], allow_small_or_imprecise_dtypes=True)
 
-    dma("y", r("at", 512, 2048), ("a", s_[:, 512:2048]), 2.4, came[:1])
+    dma("y", r("at", 1024, 2048), ("a", s_[:, 1024:2048]), 2.0, came[:1])
     dma("y", r("l2"), whole("pl"), 1.4, came)
     dma("y", r("e1t"), whole("e1"), 1.8)
     dma("y", r("wt"), whole("w"), 2.2)
@@ -285,61 +316,64 @@ def rank_program(g, core, T, topo):
     dma("y", rank("win2", me, 16), r("hall", 128 * me, 128 * me + 16), 2.7, sem="d22")
     dma("y", rank("win2s", me, 16), r("halls", 128 * me, 128 * me + 16), 2.7, sem="d22")
 
-    rst3, hold4, dbl4, down = r("cb", 64, 80), r("cb", 80, 112), r("cb", 112, 144), r("ce", 128, 256)
-    for view, c in ((r("ones"), 1.0), (r("hold32"), 1.0), (r("hold16"), 1.0), (r("rst"), 0.0), (r("pm", 0, 256, 4), 1.0), (r("mb", 0, 1), BIG),
-                    (r("cb", 0, 80), 0.0), (hold4, 1.0), (dbl4, 2.0), (r("mxs"), LOW), (r("sel"), 0.0), (down, -BIG),
-                    (r("hold32", 0, 256, 32), 0.0), (r("hold16", 0, 128, 16), 0.0), (r("rst", 0, 256, 4), LOW), (r("cb", 0, 64, 16), -1024.0),
-                    (r("cb", 67, 80, 4), LOW), (r("cb", 80, 144, 4), 0.0), (r("zt", p=quarters[0]), 0.0)):
+    hold4 = r("cb", 64, 192)
+    for view, c in ((r("ones"), 1.0), (r("hold32"), 1.0), (r("hold16"), 1.0), (r("hold8"), 1.0), (r("rst"), 0.0), (r("pm", 0, 256, 4), 0.0),
+                    (r("pm2", 0, 512, 4), 0.0), (r("won2", 0, 4), 0.0), (r("cb", 0, 64), 0.0), (hold4, 1.0), (r("sel"), 0.0),
+                    (r("hold32", 0, 256, 32), 0.0), (r("hold16", 0, 128, 16), 0.0), (r("hold8", 0, 128, 16), 0.0), (r("hold8", 8, 128, 16), 8.0),
+                    (r("rst", 0, 256, 4), LOW), (r("cb", 0, 64, 16), -1024.0), (r("cb", 64, 192, 4), 0.0)):
         op("set", view, c)
     op("ts", r15, pidx, 15, None, A.bitwise_and)
     op("ts", r31, pidx, 31, None, A.bitwise_and)
     op("ts", rq, pidx, 1, 16, A.logical_shift_right, A.bitwise_and)
     op("copy", r("ci"), r(io, 0, 128))
-    op("act", r("eidx"), r(io, 0, 256), CP, scale=1024.0 / TOP)
-    op("act", r("d1"), r(io, 0, 384), CP, scale=0.0)
+    op("act", r("d1"), r(io, 0, 256), CP, scale=0.0)
     op("act", r("k2"), r(io, 0, 128), CP, scale=64.0)
     op("copy", ip, r15)
     op("copy", sp31, r31)
-    op("ts", r("cmod"), r("ci"), 15, None, A.bitwise_and)
+    op("ts", r("cmod", 0, 128), r("ci"), 15, None, A.bitwise_and)
     op("ts", r("rsh"), r("ci", 0, 64), 1, None, A.logical_shift_right)
     op("ts", pc, rq, ip, None, A.add)
     op("ts", top0, ip, 0.5, BIG, A.add, A.mult)
     op("ts", spx, sp31, float(me), 99.0, A.is_equal, A.mult)
-    op("ts", p16k, sp31, 16.0 * 1024.0 / TOP, None, A.mult)
-    op("ts", p4k, sp31, 256.0, None, A.mult)
-    op("ts", r("mask16"), r("cmod"), ip, None, A.is_equal)
-    op("ts", r("dupo"), r("rsh", 0, 16), 16.0, ip, A.mult, A.add)
+    op("ts", t8x, sp31, 8.0, 99.0, A.is_lt, A.mult)
+    op("ts", t8, t8x, sp31, -8.0, A.add, A.add)
+    op("ts", r("mask16"), r("cmod", 0, 128), ip, None, A.is_equal)
+    op("ts", r("dupo", 0, 16), r("rsh", 0, 16), 16.0, ip, A.mult, A.add)
     op("copy", r("repo"), r("rsh"))
-    op("ts", r("swo", 0, 6, 5), r(io, 0, 32, 16), ip, None, A.add)
-    for c, b in ((1, 16.0), (3, 0.0)):
-        op("ts", r("swo", c, c + 2), r("ones", 0, 2), b, ip, A.mult, A.add)
-    for h in range(2):
-        op("copy", r("rep1", h, 8, 2), r(io, 16 * h + 3, 16 * h + 16, 4))
-        op("ts", r("esm", 16 + 4 * h, 20 + 4 * h), r(io, 0, 4), 64.0, p4k, A.mult, A.add)
     op("tt", spart, spx, sp31, A.add)
-    op("ts", r("esm", 0, 16), r(io, 0, 16), 1024.0 / TOP, p16k, A.mult, A.add)
-    op("tr", r("selt"), r("selr", 0, 32))
-    op("ts", r("selo"), r(io, 0, 16, 8), r("selt", 0, 1), None, A.add)
-    op("ts", r("mneg"), r("selr", 32, 96), pc, -1024.0, A.not_equal, A.mult)
+    op("ts", r("mneg"), r("selr"), pc, -1024.0, A.not_equal, A.mult)
 
     for t in range(4):
         op("ts", r("ubig", t, 512, 4), r("ones"), r("ut", t, t + 1), None, A.mult)
     op("quant", r("uq"), r("us"), r("ubig"))
     for a in range(2):
-        op("copy", r("offh", p=halves[a]), r("l1", 16 * a, 16 * a + 16, p=halves[a]))
-    op("act", r("kp"), by(r(io), r("offh")), CP, scale=1.0 / TOP)
-    for a in range(2):
-        op("tt", rank("key1", a), rank("kp", a), rank("eidx", a), A.add)
+        op("copy", r("offh", 0, 16, p=halves[a]), r("l1", 16 * a, 16 * a + 16, p=halves[a]))
+        op("ts", r("zi", p=halves[a]), r("l1", 16 * a, 16 * a + 16, p=halves[a]), 7, None, A.logical_shift_right)
+    op("act", r("kp"), by(r(io), r("offh", 0, 16)), CP)
+    for k in range(4):
+        op("tt", r("key1" if k == 3 else "em", k, 256, 4), r("kp", k, 256, 4), r("mask16", 0, 64), A.mult)
+    for k in range(3):
+        op("tt", r("key1", k, 256, 4), r("em", k, 256, 4), r("key1" if k == 2 else "em", k + 1, 256, 4), A.subtract)
+    op("copy", r("offh", 16, 32), r("zi"))
+    op("ts", r("pf", 16, 24), r(io, 0, 8), spart, None, A.is_equal)
+    op("act", r("wn", 0, 256), by(r("pf", 16, 24), r("offh", 16, 32)), CP)
+    op("act", r("wn", 256, 512, 4), r("wn", 1, 256, 4), CP, scale=-1.0)
+    op("ts", r("cmod", 128, 192), r("ci", 0, 64), 4, None, A.logical_shift_right)
+    op("ts", r("mk", 128, 192), r("cmod", 128, 192), t8, 2.0, A.is_gt, A.mult)
+    op("tt", r("wn", 259, 512, 4), r("wn", 3, 256, 4), r("mk", 128, 192), A.add)
+    for k in (1, 2):
+        op("tt", r("wn", 256 + k, 512, 4), r("wn", k, 256, 4), r("wn", k + 1, 256, 4), A.subtract)
+    op("ts", r64, pidx, 64, None, A.bitwise_and)
+    op("ts", ph, r64, ip, None, A.add)
+    op("ts", r("dupo", 16, 24), r("dupo", 0, 8), 4.0, 3.0, A.mult, A.add)
     op("copy", r("offo"), r("lo"))
     for a in range(2):
         op("act", rank("er2", a, 256), by(r(io), rank("offo", a, 16)), CP)
-    op("tt", r("ew2", 128, 192), r("kp", 0, 256, 4), r("mask16", 0, 64), A.mult)
-    op("scan", r("es2", 128, 192), r("hold16", 0, 64), r("ew2", 128, 192), 0.0, A.mult, A.add)
-    etab, etab2 = r("f8", 0, 4), r("es2", 15, 128, 16)
-    op("ts", etab, r("es2", 143, 192, 16), TOP, None, A.mult)
+    op("scan", r("es2", 128, 192), r("hold16", 0, 64), r("em", 0, 256, 4), 0.0, A.mult, A.add)
+    etab, etab2 = r("es2", 143, 192, 16), r("es2", 15, 128, 16)
     for a in range(2):
         op("tt", rank("ew2", a, 64), r("er2", 256 * a, 256 * a + 256, 4), r("mask16", 0, 64), A.mult)
-    op("scan", r("es2", 0, 128), r("hold16"), r("ew2", 0, 128), 0.0, A.mult, A.add)
+    op("scan", r("es2", 0, 128), r("hold16"), r("ew2"), 0.0, A.mult, A.add)
     for i in range(4):
         op("quant", rank("aq", i), rank("asc", i), rank("at", i, 512))
     op("quant", r("wq"), r("ws"), r("wt"))
@@ -350,8 +384,8 @@ def rank_program(g, core, T, topo):
     def i8(i):
         return rank("i8", i, 8)
 
-    def mm(out, w, x):
-        return op("mm", out, w[0], w[1], x[0], x[1], True, True)
+    def mm(out, w, x, behind=()):
+        return op("mm", out, w[0], w[1], x[0], x[1], True, True, behind=behind)
 
     U = r("uq"), r("us")
 
@@ -369,43 +403,51 @@ def rank_program(g, core, T, topo):
         op("scan", rank("mx", i), rank("rst", i), rank("gv", i), 0.0, A.add, A.max)
         for k in (1, 2, 3):
             a, e = 128 * i + k, 128 * i + 128
-            op("tt", r("pm", a, e, 4), r("gv", a, e, 4), r("mx", a - 1, e, 4), A.is_gt)
-        op("scan", rank("st1", i), rank("pm", i), rank("key1", i), 0.0, A.max, A.min)
+            op("tt", r("pm", a, e, 4), r("gv", a, e, 4), r("mx", a - 1, e, 4), A.is_le)
+        op("scan", rank("wn", 4 + i), rank("pm", i), rank("wn", 2 + i), 0.0, A.mult, A.add)
+        op("scan", rank("st1", i), rank("pm", i), rank("key1", i), 0.0, A.mult, A.add)
 
-    keys, chosen, th = r("st1", 3, 256, 4), r("i8", 36, 40), r("mk", 192, 256)
-    op("ts", r("zi", 0, 64), keys, TOP, None, A.mult)
-    op("ts", r("zi", 64, 128), r("zi", 0, 64), 7, 7, A.logical_shift_right, A.bitwise_and)
-    op("ts", th, r("zi", 64, 128), spart, 1.0e6, A.not_equal, A.mult)
-    op("ts", r("mk", 128, 192), r("zi", 64, 128), spart, None, A.is_equal)
-    op("act", r("dup1"), by(th, r("dupo", 0, 8)), CP)
+    def spread(out, name, a, b, step, add=0.0):
+        for i, to in enumerate(halves):
+            for there in halves:
+                op("ts", r("cu1", out + 4 * i, out + 4 * i + 4, p=there), r(name, a, b, step, to), add, None, A.add)
+
+    chosen = r("cs", 143, 192, 16)
+    op("scan", r("cs", 128, 192), r("hold16", 0, 64), r("st1", 3, 256, 4), 0.0, A.mult, A.add)
+    spread(8, "cs", 143, 192, 16)
+    spread(16, "es2", 143, 192, 16, -128.0 * me)
+    op("act", rank("x1s", 0), by(r("halls"), r("cu1", 8, 16)), CP)
+    op("copy", rank("x1", 0), by(r("hall"), r("cu1", 8, 16)))
+    op("act", rank("x1s", 1), by(rank("halls", me), r("cu1", 16, 24)), CP)
+    op("copy", rank("x1", 1), by(rank("hall", me), r("cu1", 16, 24)))
+    op("act", r("dup1"), by(r("wn", 512, 768), r("dupo", 16, 24)), IDN, bias=1.0e6, scale=-1.0e6)
     for out in (r("cum1", 64, 128, p=halves[1]), r("cum1", 0, 64, p=halves[0])):
-        op("scan", out, r("ones", 0, 64, p=halves[0]), r("mk", 128, 192, p=halves[0]), -16.5, A.mult, A.add)
-    op("scan", r("cum1", 0, 64, p=halves[1]), r("ones", 0, 64, p=halves[1]), r("mk", 128, 192, p=halves[1]), r("cum1", 127, 128, p=halves[1]),
+        op("scan", out, r("ones", 0, 64, p=halves[0]), r("wn", 515, 768, 4, halves[0]), -16.5, A.mult, A.add)
+    op("scan", r("cum1", 0, 64, p=halves[1]), r("ones", 0, 64, p=halves[1]), r("wn", 515, 768, 4, halves[1]), r("cum1", 127, 128, p=halves[1]),
        A.mult, A.add)
-    op("scan", r("cs", 128, 192), r("mask16", 0, 64), keys, 0.0, A.max, A.min)
-    op("ts", r("i8", 32, 36), r("cs", 143, 192, 16), TOP, None, A.mult)
-    op("ts", chosen, r("i8", 32, 36), 1023, None, A.bitwise_and)
-    op("copy", r("sel", 1, 9, 2), chosen)
-    op("tt", r("sel", 0, 8, 2), etab, chosen, A.subtract)
     op("tt", r("v1"), by(r("cum1", 0, 64), r("dupo", 0, 8)), r("dup1"), A.is_gt)
     op("tr", r("vt1"), r("v1"))
-    op("scan", r("vs1"), r("hold16"), r("vt1"), 0.0, A.mult, A.add)
-    op("scan", r("sel", 16, 24), r("vs1", 15, 128, 16), r("sel", 1, 9), r("sel", 0, 1), A.mult, A.add)
-    for a, to in enumerate(halves):
+    op("scan", rank("vs1", 0), r("hold8"), r("vt1"), 0.0, A.mult, A.add)
+    for i, to in enumerate(halves):
         for there in halves:
-            op("copy", r("cu1", 4 * a, 4 * a + 4, p=there), r("sel", 16, 24, 2, p=to))
-    op("act", r("x1s"), by(r("halls"), r("cu1")), CP)
-    op("copy", r("x1"), by(r("hall"), r("cu1")))
+            op("ts", r("cu1", 24 + 4 * i, 28 + 4 * i, p=there), r("vs1", 15, 128, 32, to), 16.0, r("pf", 8, 9, p=to), A.mult, A.add)
+    op("scan", rank("vs1", 1), r("hold16"), r("vt1"), 0.0, A.mult, A.add)
+    op("copy", r("sel", 1, 9, 2), chosen)
+    op("tt", r("sel", 0, 8, 2), etab, chosen, A.subtract)
+    op("scan", r("sel", 16, 24), r("vs1", 135, 256, 16), r("sel", 1, 9), r("sel", 0, 1), A.mult, A.add)
+    spread(0, "sel", 16, 24, 2)
 
     def products(out, X):
+        m, a = [], []
         for i in range(4):
-            mm(r("pr", 512 * i, 512 * i + 128), (rank("aq", i), rank("asc", i)), X)
-            op("act", out(i), r("pr", 512 * i, 512 * i + 128), CP, scale=0.05)
+            m = [mm(r("pr", 512 * i, 512 * i + 128), (rank("aq", i), rank("asc", i)), X, m)]
+            a = [op("act", out(i), r("pr", 512 * i, 512 * i + 128), CP, behind=a, scale=0.05)]
 
-    products(lambda i: rank("hs1", i), (r("x1"), r("x1s")))
-    op("act", r("base1"), by(r("sc"), r("cu1")), CP)
+    for h in (1, 0):
+        products(lambda i: rank("hs1", 2 * i + h), (rank("x1", h), rank("x1s", h)))
+    op("act", r("base1"), by(r("sc"), r("cu1", 0, 8)), CP)
     for i in range(4):
-        op("tt", r("h1", i, 512, 4), rank("hs1", i), r("e1t", i, 512, 4), A.add)
+        op("tt", r("h1", i, 512, 4), by(rank("hs1", i, 256), r("cu1", 24, 32)), r("e1t", i, 512, 4), A.add)
     H1 = r("h1q"), r("h1s")
     op("quant", H1[0], H1[1], r("h1"))
 
@@ -418,39 +460,39 @@ def rank_program(g, core, T, topo):
     arrive("ae", count(SCORES), [rank("sp", s, 4) for s in range(N) if s != me], sent)
     op("tt", rank("sc2", me), r("ps", 0, 128), r("base1"), A.add)
     products(lambda i: rank("rs", 2 * i + 1), H1)
-    op("act", r("chr1"), by(r(io), r("cu1")), CP)
-    dma("y", ("ch", s_[0:1, :]), r("chr1", p=slice(0, 1)), 1.2, [sent], "d23")
+    op("act", rank("chr", 0), by(r(io), r("cu1", 0, 8)), CP)
+    dma("y", ("ch", s_[0:1, :]), r("chr", 0, 128, p=slice(0, 1)), 1.2, [sent], "d23")
 
-    def sf(i):
-        return rank("sf", i, 32)
+    op("copy", r("off2", 0, 32), r("l2"))
+    op("ts", r("si"), r("l2"), 7, None, A.logical_shift_right)
+    op("copy", r("off2", 32, 64), r("si"))
+    op("ts", r("pf", 24, 32), r(io, 0, 8), float(me), BIG, A.is_equal, A.mult)
+    for s in range(N):
+        op("act", rank("wcol", s), r(io, 0, 128), CP, scale=0.5 if s == me else 0.0)
+    for h in range(4):
+        op("act", rank("hm2", h), by(r("pf", 24, 32), rank("off2", 4 + h, 8)), CP)
+        op("act", rank("col2", h), by(r("wcol"), rank("off2", h, 8)), CP)
+    op("act", r("cw2", 0, 512, 4), r("hm2", 1, 512, 4), CP, scale=-1.0)
+    op("act", r("cw2", 3, 512, 4), r("hm2", 3, 512, 4), CP)
+    op("act", r("col2", 0, 512, 4), r("k2"), CP)
+    q0 = quarters[0]
+    op("act", r("ce2", 3, 512, 4, q0), r("er2", 3, 512, 4, q0), CP)
+    for h in range(2):
+        a, e = 256 * h, 256 * h + 256
+        for k in (1, 2):
+            op("tt", r("cw2", a + k, e, 4), r("hm2", a + k, e, 4), r("hm2", a + k + 1, e, 4), A.subtract)
+        for k in range(3):
+            op("tt", r("ce2", a + k, e, 4, q0), r("er2", a + k, e, 4, q0), r("er2", a + k + 1, e, 4, q0), A.subtract)
+    for h in range(4):
+        op("scan", rank("k1", h), hold4, rank("col2", h), 0.0, A.mult, A.add)
 
-    def si(i):
-        return rank("si", i, 32)
-
-    op("copy", r("lf"), by(r("l2"), r("swo")))
-    op("tr", r("lt3"), r("lf"))
-    op("copy", si(0), r("lt3", 0, 32))
-    op("copy", r("off2"), by(r("lt3"), r("selo")))
-    op("ts", si(1), si(0), 7, None, A.logical_shift_right)
-    op("ts", si(2), si(0), 127, None, A.bitwise_and)
-    op("ts", r("sf", 128, 144), r("lt3", 0, 16), 1.0 / TOP, None, A.mult)
-    op("ts", sf(0), si(1), float(me), 0.5, A.is_equal, A.mult)
-    op("tt", r("sf", 160, 176), r("sf", 128, 144), r("esm", 0, 16), A.add)
-    op("tt", sf(2), si(2), sf(0), A.mult)
-    op("scan", sf(1), dbl4, sf(0), 0.0, A.mult, A.add)
-    op("scan", sf(3), hold4, sf(2), 0.0, A.mult, A.add)
-    op("tt", r("sf", 99, 128, 4), r("sf", 99, 128, 4), r("esm", 16, 24), A.add)
-    op("act", r("k1r"), by(sf(3), r("rep1")), CP)
-    for a in range(4):
-        op("tr", r("k1", a, 128, 4), rank("k1r", a, 32))
-
-    cut = [q for q in (1, 2, 3) if q == 1 or (me + q) % N == 0] + [4]
-    for a, b in zip(cut, cut[1:]):
-        op("copy", r("d1", 128 * a - 128, 128 * b - 128, 32), r("sp", 4 * ((me + a) % N), 4 * ((me + a) % N + b - a)))
     for q in range(1, N):
         s = (me + q) % N
-        if q < 4:
-            op("scan", rank("rp", s), r("hold32", 0, 128), rank("d1", q - 1), 0.0, A.mult, A.add)
+        if q == 1:
+            op("copy", rank("rp", s), by(r("sp"), rank("repo", s, 8)))
+        elif q < 4:
+            op("copy", r("d1", 128 * q - 256, 128 * q - 128, 32), rank("sp", s, 4))
+            op("scan", rank("rp", s), r("hold32", 0, 128), rank("d1", q - 2), 0.0, A.mult, A.add)
         else:
             op("act", rank("rp", s), by(r("sp"), rank("repo", s, 8)), CP)
         op("tr", rank("sc2", s), rank("rp", s))
@@ -459,18 +501,14 @@ def rank_program(g, core, T, topo):
         op("copy", rank("gw", h), by(r("sc2"), rank("off2", h, 8)))
         op("act", rank("gw", 2 + h), by(r("sc2"), rank("off2", 2 + h, 8)), CP)
     for h in (0, 2, 1, 3):
-        op("tr", rank("gT", h), rank("gw", h))
-    for h in range(2):
-        op("scan", r("mxs", 17 * h + 1, 17 * h + 17), r("gT", 16 * h, 512, 32), rst3, LOW, A.max, A.add)
-        op("tt", rank("pms", h, 16), r("gT", 16 * h, 512, 32), r("mxs", 17 * h, 17 * h + 16), A.is_gt)
-        op("scan", rank("kk", h, 16), rank("pms", h, 16), r("sf", 32 + 16 * h, 48 + 16 * h), 0.0, A.max, A.min)
-    op("ts", r("fl", 0, 64), by(r("kk"), r("rep1", 0, 4)), 0.5, BIG, A.not_equal, A.mult)
-    op("act", r("fl", 64, 128), by(r("kk"), r("rep1", 4, 8)), ABS, bias=-BIG, scale=2.0 * BIG)
-    for a in range(4):
-        op("tr", r("mb", 1 + a, 129, 4), rank("fl", a, 32))
-    op("scan", r("ce", 0, 128), down, r("mb", 0, 128), top0, A.add, A.add)
-    op("scan", rank("ks", 0), r("ce", 0, 128), r("k1"), 0.0, A.max, A.min)
-    op("scan", rank("ks", 1), r("ce", 0, 128), r("k2"), 0.0, A.max, A.min)
+        op("scan", rank("mx2", h), r("rst", 0, 128), rank("gw", h), 0.0, A.add, A.max)
+        for k in (1, 2, 3):
+            a, e = 128 * h + k, 128 * h + 128
+            op("tt", r("pm2", a, e, 4), r("gw", a, e, 4), r("mx2", a - 1, e, 4), A.is_le)
+        op("scan", r("won2", 128 * h + 4, 128 * h + 132), rank("pm2", h), rank("cw2", h), 0.0, A.mult, A.add)
+    op("scan", r("ce"), r("ones"), r("won2", 3, 512, 4), top0, A.mult, A.subtract)
+    op("scan", rank("ks", 0), r("ce"), r("k1", 3, 512, 4), 0.0, A.max, A.min)
+    op("scan", rank("ks", 1), r("ce"), r("k2"), 0.0, A.max, A.min)
     op("ts", r("lr"), r("mneg"), r("ks", 127, 128), r("ks", 255, 256), A.add, A.subtract)
     op("tr", r("lt"), r("lr"))
     for there in halves:
@@ -489,23 +527,24 @@ def rank_program(g, core, T, topo):
         sent = send(far(T, topo, core, me, share, "a2", src, dst), [], [sent])
     arrive("a2", count(*PICKS) + 2 * count(*PICKS_H), [rank(n, s, 16) for s in range(N) if s != me for n in ("win2", "win2s")], first)
 
-    q0 = quarters[0]
-    op("scan", r("zt", 8, 136, 8, q0), r("pms", 0, 16, p=q0), r("sf", 160, 176, p=q0), 0.0, A.max, A.min)
-    for a in range(4):
-        op("tr", r("zrow", a, 128, 4, q0), r("zt", 32 * a + 32, 32 * a + 64, p=q0))
-    op("bc", r("zf2"), r("zrow", p=slice(0, 1)), 128)
-    cnt, mk = r("vs", 31, 256, 32), r("mk", 0, 128)
-    op("ts", r("zb2"), r("zf2"), TOP, None, A.mult)
-    op("scan", r("cs", 0, 128), r("mask16"), r("zf2"), 0.0, A.max, A.min)
-    op("ts", r("sj"), r("zb2"), 7, 7, A.logical_shift_right, A.bitwise_and)
-    op("ts", i8(0), r("cs", 15, 128, 16), TOP, None, A.mult)
+    for h in range(4):
+        op("scan", r("e2s", 128 * h, 128 * h + 128, p=q0), r("pm2", 128 * h, 128 * h + 128, p=q0), r("ce2", 128 * h, 128 * h + 128, p=q0), 0.0,
+           A.mult, A.add)
+    op("act", r("zf2", 128, 256, p=slice(0, 1)), r("e2s", 3, 512, 4, slice(0, 1)), CP)
+    op("bc", rank("zf2", 0), r("zf2", 128, 256, p=slice(0, 1)), 128)
+    cnt, mk, c2 = r("vs", 31, 256, 32), r("mk", 0, 128), r("cs", 15, 128, 16)
+    op("copy", r("zb2"), rank("zf2", 0))
+    for h in range(2):
+        op("tt", rank("base2", h, 64), rank("zf2", h, 64), r("mask16", 0, 64), A.mult)
+    op("scan", r("cs", 0, 128), r("hold16"), r("base2"), 0.0, A.mult, A.add)
+    op("ts", r("sj"), r("zb2"), 7, None, A.logical_shift_right)
     op("ts", mk, r("sj"), spart, None, A.is_equal)
-    op("act", r("dup2"), by(mk, r("dupo")), CP)
-    op("ts", i8(2), i8(0), 1023, None, A.bitwise_and)
+    op("act", r("dup2"), by(mk, r("dupo", 0, 16)), CP)
+    op("copy", i8(2), c2)
     op("scan", r("cum"), r("ones"), mk, 0.0, A.mult, A.add)
-    op("ts", f8(4), i8(2), float(128 - 128 * me), None, A.add)
+    op("ts", f8(4), c2, float(128 - 128 * me), None, A.add)
     op("ts", i8(3), i8(2), 7, None, A.logical_shift_right)
-    op("tt", f8(5), etab2, i8(2), A.subtract)
+    op("tt", f8(5), etab2, c2, A.subtract)
     for h in range(2):
         op("tt", rank("v2", h), by(r("cum"), rank("dupo", h, 8)), rank("dup2", h), A.mult)
     op("ts", f8(6), i8(3), 16.0, -1.0, A.mult, A.add)
@@ -519,13 +558,13 @@ def rank_program(g, core, T, topo):
     op("tt", f8(11), f8(9), f8(8), A.subtract)
     op("tt", f8(14), f8(12), f8(4), A.add)
     op("tt", f8(13), f8(11), f8(10), A.mult)
-    op("tt", f8(16), f8(12), i8(2), A.add)
+    op("tt", f8(16), f8(12), c2, A.add)
     op("tt", f8(15), f8(13), f8(14), A.add)
     op("copy", r("cu2"), f8(16))
     op("copy", r("ixu"), f8(15))
     op("act", r("base2"), by(r("sc2"), r("cu2")), CP)
-    op("act", r("chr2"), by(r(io), r("cu2")), CP)
-    dma("y", ("ch", s_[1:2, :]), r("chr2", p=slice(0, 1)), 1.2, sem="d23")
+    op("act", rank("chr", 1), by(r(io), r("cu2")), CP)
+    dma("y", ("ch", s_[1:2, :]), r("chr", 128, 256, p=slice(0, 1)), 1.2, sem="d23")
 
     products(lambda i: rank("rs", 2 * i), (r("win2"), r("win2s")))
     for i in range(4):
@@ -543,7 +582,9 @@ def rank_program(g, core, T, topo):
     dma("s", whole("y"), r("yt"), 1.4, sem="d23")
     dma("y", whole("g"), r("gout", p=slice(0, 1)), 1.2, sem="d23")
 
-    seq = order(steps)
+    if not ORDER:
+        ORDER.extend(order(steps))
+    seq = ORDER
     total, upto = {}, {}
     for i in seq:
         s = steps[i]

import numpy as np
from concourse.bass import DstId, RemoteDMATransfer
from concourse.mybir import dt, AluOpType, ActivationFunctionType

X4 = "float8_e4m3fn_x4"
F, B, I, U16, U8 = "float32", "bfloat16", "int32", "uint16", "uint8"
SIZES = {
    B: dict(e0t=512, e1t=512, e2t=512, at=2048, wt=512, ut=4, ubig=512, ones=128, hold32=256, hold16=128, rst=256, cb=192, mask16=128,
            mneg=64, k2=128, pm=256, wn=768, mk=192, cum=128, cum1=128, dup1=128, dup2=256, v1=128, vt1=128, vs1=256, v2=256,
            vt=256, vs=256, pm2=512, hm2=512, cw2=512, won2=520, ce=128, hold8=128, lr=64, lt=64, ls=128, r8=8, h1=512, h2=512),
    F: dict(pf=32, io1=1024, em=256, selr=64, er2=512, ce2=512, e2s=512, wcol=1024, col2=512, k1=512, mx2=512, kp=256, key1=256,
            st1=256, ew2=128, es2=192, sc=1024, gv=256, gw=512, mx=256, sel=24, cs=192, f8=160, base1=128, bt=128, gt=128, sp=32,
            d1=256, rp=1024, sc2=1024, base2=128, gout=128, yt=128, zf2=256, ks=256, chr=256, hs1=1024, rs=1024),
    I: dict(l1=32, lo=32, l2=32, pi=8, ci=128, cmod=192, rsh=64, zi=16, zb2=128, sj=128, i8=32, si=32),
    U16: dict(repo=64, dupo=24, offo=32, offh=32, cu1=32, cu2=8, off2=64, offp=8, ixu=8),
    X4: dict(uq=128, aq=512, wq=128, hall=1024, x1=256, h1q=128, pk=128, win2=128, h2q=128),
    U8: dict(us=128, asc=512, ws=128, halls=1024, x1s=256, h1s=128, pks=128, win2s=128, h2s=128),
}
SCRATCH = {name: ("sbuf", [128, n], d) for d, names in SIZES.items() for name, n in names.items()}
SCRATCH.update({"pst": ("dram", [128, 4], I), "pl": ("dram", [8, 128, 4], I),
                "ps": ("psum", [128, 2048], F), "pr": ("psum", [128, 2048], F)})

REMOTE = ["al", "a0a", "a0b", "a0h", "a0i", "ae", "a2", "left", "hl", "hc", "kc", "ks"]
SEMAPHORES = REMOTE + ["qv", "qs", "qt", "qg"] + ["d%d" % i for i in range(24)]
A = AluOpType
CP, IDN = ActivationFunctionType.Copy, ActivationFunctionType.Identity
LOW = -1.0e29
BIG = 16384.0
s_ = np.s_

TIERS = (("a0a", {1: 4, 2: 4}), ("a0b", {3: 4, 4: 4}))
TIERS_H = (("a0h", {5: 4, 6: 4}), ("a0i", {7: 8}))
LISTS = ({1: 2, 2: 2, 3: 2, 4: 2}, {5: 2, 6: 2, 7: 4})
SCORES = {q: 1 for q in range(1, 8)}
PICKS = ({1: 2, 2: 2, 3: 4}, {3: 4, 1: 2, 2: 2})
PICKS_H = ({4: 4, 5: 4}, {6: 4, 7: 4})

WAIT, CYCLE, SLACK, TRIES = 0.18, 0.001, 0.03, 1200
CASES = ((0.14, 1.0, 1.15), (0.2, 0.9, 1.05), (0.17, 1.0, 0.8), (0.16, 1.2, 1.0))
LAG = {"a0a": 2.2, "a0h": 3.7, "a0i": 4.3, "a0b": 3.8, "al": 3.0, "ae": 1.8, "a2": 2.6}
ORDER = []


def helpers(core, topo):
    return [c for c in topo.cores_of(core) if topo.die(c) != topo.die(core)][:len(LISTS)]


def fused(g, T, topo, core, parts):
    tr = []
    for c, e, sem, src, dst in parts:
        rid, pid = topo.addr(c, core)
        tr.append(RemoteDMATransfer(dst_ids=[DstId(rid=rid, pnc=pid)], dma_engine_mask=sum(1 << x for x in e), remote_sem=T.sem[sem],
                                    srcs=[src], dsts=[dst]))
    g.remote_dma_fused(tr, local_sem=T.sem.left)
    return sum(len(e) for c, e, sem, src, dst in parts)


def far(T, topo, core, me, share, sem, src, dst):
    parts, at = [], 0
    for q, n in share.items():
        d = (me + q) % len(T.cores)
        parts.append((T.cores[d], topo.engines(core, T.cores[d])[at:at + n], sem, src(q), dst(d)))
        at += n
    return parts


def inner(T, topo, core, me):
    away = topo.engines(core, T.cores[(me + 1) % len(T.cores)])
    return [x for x in topo.engines(core, helpers(core, topo)[0]) if x not in away]


def near(T, topo, core, me, sem, src, n=None):
    hp, e = helpers(core, topo), inner(T, topo, core, me)
    m = len(e) // len(hp)
    return [(c, e[m * i:m * i + (n or m)], sem, src(i), src(i)) for i, c in enumerate(hp)]


def columns0(T, me):
    mine = slice(128 * me, 128 * me + 128)
    return T.hall[:, mine].bitcast(dt.uint8), T.halls[:, mine]


def pick_calls(T, me):
    land = slice(16 * me, 16 * me + 16)
    return (("kc", lambda q: T.pk[:, 16 * q:16 * q + 16].bitcast(dt.uint8), lambda d: T.win2[:, land].bitcast(dt.uint8)),
            ("ks", lambda q: T.pks[:, 16 * q:16 * q + 16], lambda d: T.win2s[:, land]))


def helper_program(g, core, T, topo, me, k):
    N, own = len(T.cores), T.cores[me]
    g.wait_ge(T.sem.hl, 1)
    left = fused(g, T, topo, core, far(T, topo, core, me, LISTS[k], "al", lambda q: T.pst[:], lambda d: T.pl[(me - d) % N]))
    g.wait_ge(T.sem.hc, len(inner(T, topo, own, me)))
    piece = columns0(T, me)[k]
    for sem, share in TIERS_H:
        left += fused(g, T, topo, core, far(T, topo, core, me, share, sem, lambda q: piece, lambda d: piece))
    n = len(near(T, topo, own, me, "kc", lambda i: None)[k][1])
    for sem, src, dst in pick_calls(T, me):
        g.wait_ge(T.sem[sem], n)
        left += fused(g, T, topo, core, far(T, topo, core, me, PICKS_H[k], "a2", src, dst))
    g.wait_ge(T.sem.left, left)


def place(view):
    name, ix = view
    where, shape, d = SCRATCH[name]
    if where == "dram":
        return name, 1, 1 << ix if isinstance(ix, int) else -1
    p, c = range(*ix[0].indices(128)), range(*ix[1].indices(shape[1]))
    if where == "psum":
        return name, 1, 1 << c[0] // 512
    return name, sum(1 << x for x in p), sum(1 << x for x in c)


def width(view):
    return len(range(*view[1][1].indices(SCRATCH[view[0]][1][1])))


def order(steps):
    n = len(steps)
    q, time, lag = [[s[k] for s in steps] for k in ("q", "time", "lag")]
    deps, behind = [s["deps"] for s in steps], [s["behind"] for s in steps]
    after = [[] for s in steps]
    for i in range(n):
        for d in deps[i] + behind[i]:
            after[d].append(i)
    rest = [0.0] * n
    for i in range(n - 1, -1, -1):
        rest[i] = max([time[i] + rest[j] if i in behind[j] else lag[i] + WAIT + rest[j] for j in after[i]] + [lag[i]])

    def lay(way):
        open_ = [len(deps[i]) + len(behind[i]) for i in range(n)]
        ready, since, free, out = {}, [0.0] * n, {}, []
        for i in range(n):
            if not open_[i]:
                ready.setdefault(q[i], []).append(i)
        while len(out) < n:
            best = None
            for k, mine in ready.items():
                f = free.get(k, 0.0)
                while mine:
                    top = max(mine, key=lambda i: way[i])
                    t = max(f, since[top])
                    mine = [i for i in mine if since[i] < t and f < t and max(f, since[i]) + time[i] <= t + SLACK]
                    pick = t, top
                if ready[k] and (best is None or pick < best):
                    best = pick
            t, i = best
            ready[q[i]].remove(i)
            out.append(i)
            if q[i]:
                free[q[i]] = t + time[i]
            for j in after[i]:
                since[j] = max(since[j], t + time[i] if i in behind[j] else t + lag[i] + WAIT)
                open_[j] -= 1
                if not open_[j]:
                    ready.setdefault(q[j], []).append(j)
        return out

    def span(seq):
        total = 0.0
        for wait, work, away in CASES:
            start, free = [0.0] * n, {}
            took = [lag[i] * (work if lag[i] == time[i] else away) for i in range(n)]
            for i in seq:
                start[i] = max([free.get(q[i], 0.0)] + [start[d] + took[d] + wait for d in deps[i]] + [start[d] + time[d] for d in behind[i]])
                if q[i]:
                    free[q[i]] = start[i] + time[i] * work
            total += max(start[i] + took[i] for i in range(n))
        return total

    rng = np.random.RandomState(0)
    way = [x - 1e-6 * i for i, x in enumerate(rest)]
    seq = lay(way)
    least = span(seq)
    for k in range(TRIES):
        other = list(way)
        for i in rng.randint(0, n, 1 + k % 12):
            other[i] += float(rng.normal()) * 0.4
        s = lay(other)
        t = span(s)
        if t < least:
            way, seq, least = other, s, t
    return seq


def rank_program(g, core, T, topo):
    me = T.rank_of(core)
    if me is None:
        for r, c in enumerate(T.cores):
            if core in helpers(c, topo):
                helper_program(g, core, T, topo, r, helpers(c, topo).index(core))
        return
    N = len(T.cores)
    Q = {"g": g, "v": g.vector, "s": g.scalar, "t": g.tensor, "y": g.sync}
    steps, seen_by = [], {}

    def add(q, call, reads, writes, time, lag=None, sem=None, count=1, deps=(), behind=()):
        deps = set(deps)
        i = len(steps)
        for views, wr in ((reads, False), (writes, True)):
            for view in views:
                if view[0] not in SCRATCH:
                    continue
                name, p, c = place(view)
                w1 = wr or name in ("ps", "pr")
                for j, w2, p2, c2 in seen_by.setdefault(name, []):
                    if (w1 or w2) and p & p2 and c & c2 and j != i:
                        deps.add(j)
                seen_by[name].append((i, w1, p, c))
        behind = list(behind) + [j for j in deps if steps[j]["sem"] == "left"] + [j for j in range(i) if q == steps[j]["q"] == "y"][-1:]
        steps.append(dict(q=q, call=call, deps=sorted(deps - set(behind)), behind=behind, time=time, lag=time if lag is None else lag,
                          sem=sem or "q" + q, count=count))
        return i

    def ap(x, cast=None):
        if not isinstance(x, tuple):
            return x
        a = T[x[0]][x[1]]
        if cast is not None and SCRATCH.get(x[0], "...")[2] == X4:
            a = a.bitcast(cast)
        return a.indirect(ap(x[2])) if len(x) == 3 else a

    F_ = {"copy": g.vector.tensor_copy, "tt": g.vector.tensor_tensor, "ts": g.vector.tensor_scalar, "set": g.vector.memset,
          "scan": g.vector.tensor_tensor_scan, "tr": g.vector.transpose, "quant": g.vector.quantize_mx,
          "mm": g.tensor.matmul_mx, "act": g.scalar.activation, "iota": g.iota, "bc": g.partition_broadcast}

    def op(name, *args, deps=(), behind=(), **kw):
        q = {"mm": "t", "act": "s", "iota": "g", "bc": "g"}.get(name, "v")
        views = [a for a in args if isinstance(a, tuple)]
        outs = 2 if name == "quant" else 1
        reads = [a[:2] for a in views[outs:]] + [a[2] for a in views if len(a) == 3]
        n = width(views[0])
        if any(len(a) == 3 for a in views):
            time = 0.065 + 1.5 * n * CYCLE
        elif name in ("quant", "mm", "iota", "bc"):
            time = {"quant": 0.15, "mm": 0.13, "iota": 0.16 + 2 * n * CYCLE, "bc": 0.17 + 4 * n * CYCLE}[name]
        else:
            short = all(SCRATCH[a[0]][2] in (B, U16) for a in views if width(a) == n) and name != "act"
            both = name == "tt" and not any(a[0] in ("ps", "pr") for a in views)
            time = max(64, n * (2 if both else 0.5 if short else 1)) * CYCLE + (0.03 if q == "s" else 0)
        cast = dt.uint32 if name == "copy" else None
        return add(q, lambda: F_[name](*[ap(a, cast) for a in args], **kw), reads, views[:outs], time, deps=deps, behind=behind)

    used = [0]

    def dma(q, out, in_, lag, deps=(), sem=None):
        if sem is None:
            used[0] += 1
            sem = "d%d" % (used[0] - 1)
        return add(q, lambda: Q[q].dma_start(ap(out, dt.uint8), ap(in_, dt.uint8)), [in_], [out], 0.05, lag, sem, 16, deps)

    left = [0]

    def send(parts, reads, deps=(), time=0.15):
        left[0] += sum(len(p[1]) for p in parts)
        return add("g", lambda: fused(g, T, topo, core, parts), reads, [], time, sem="left", count=0, deps=deps)

    def arrive(sem, count, writes, sent):
        return add(None, None, [], writes, 0.0, LAG[sem], sem, count, [sent])

    def count(*shares):
        return sum(n for share in shares for n in share.values())

    def r(name, a=None, b=None, step=None, p=slice(None)):
        return name, (p, slice(a, b, step))

    def by(win, off):
        return win + (off,)

    def whole(name):
        return name, s_[:]

    def rank(name, s, n=128):
        return r(name, n * s, n * s + n)

    halves = slice(0, 64), slice(64, 128)
    quarters = [slice(32 * a, 32 * a + 32) for a in range(4)]
    io = "io1"

    dma("y", r("e0t"), whole("e0"), 1.4)
    dma("s", whole("pst"), whole("p2"), 1.0)
    dma("s", r("ut"), ("u", s_[:, 0:4]), 1.5)
    dma("s", ("pl", 0), whole("p2"), 1.5)
    for k in range(8):
        dma("y", r("l1", p=slice(16 * k, 16 * k + 16)), whole("p1"), 1.3, sem="d20")
    dma("y", r("at", 0, 1024), ("a", s_[:, 0:1024]), 2.2)
    for k in range(8):
        dma("y", r("lo", p=slice(16 * k, 16 * k + 16)), whole("p2"), 1.6, sem="d21")

    pidx, r15, r31, rq, r64 = [r("pi", i, i + 1) for i in range(5)]
    ip, sp31, spx, spart, pc, t8, t8x, top0, ph = [r("pf", i, i + 1) for i in range(9)]
    op("iota", pidx, [[0, 1]], 0, 1)
    op("iota", r(io, 0, 128), [[1, 128]], 0, 0, allow_small_or_imprecise_dtypes=True)
    for k in range(1, 8):
        op("act", rank(io, k), r(io, 0, 128), IDN, bias=float(128 * k))

    sent = send(near(T, topo, core, me, "hl", lambda i: T.pst[:], 1), [whole("pst")], time=0.9)
    arrive("al", count(*LISTS), [("pl", q) for q in range(1, N)], sent)
    op("quant", rank("hall", me), rank("halls", me), r("e0t"))
    for c, piece, name in zip(helpers(core, topo), columns0(T, me), ("hall", "halls")):
        sent = send([(c, inner(T, topo, core, me), "hc", piece, piece)]
                    + far(T, topo, core, me, TIERS[0][1], TIERS[0][0], lambda q: piece, lambda d: piece), [rank(name, me)], [sent])
    first = sent
    for piece in columns0(T, me):
        sent = send(far(T, topo, core, me, TIERS[1][1], TIERS[1][0], lambda q: piece, lambda d: piece), [], [sent])
    tiers = (TIERS[0], TIERS_H[0], TIERS_H[1], TIERS[1])
    came = [arrive(sem, 2 * count(share), [rank(n, (me - q) % N) for q in share for n in ("hall", "halls")], first) for sem, share in tiers]
    op("iota", r("selr"), [[16, 2], [0, 2], [1, 16]], 0, 0, deps=[sent], allow_small_or_imprecise_dtypes=True)

    dma("y", r("at", 1024, 2048), ("a", s_[:, 1024:2048]), 2.0, came[:1])
    dma("y", r("l2"), whole("pl"), 1.4, came)
    dma("y", r("e1t"), whole("e1"), 1.8)
    dma("y", r("wt"), whole("w"), 2.2)
    dma("y", r("e2t"), whole("e2"), 2.6)
    dma("y", rank("win2", me, 16), r("hall", 128 * me, 128 * me + 16), 2.7, sem="d22")
    dma("y", rank("win2s", me, 16), r("halls", 128 * me, 128 * me + 16), 2.7, sem="d22")

    hold4 = r("cb", 64, 192)
    for view, c in ((r("ones"), 1.0), (r("hold32"), 1.0), (r("hold16"), 1.0), (r("hold8"), 1.0), (r("rst"), 0.0), (r("pm", 0, 256, 4), 0.0),
                    (r("pm2", 0, 512, 4), 0.0), (r("won2", 0, 4), 0.0), (r("cb", 0, 64), 0.0), (hold4, 1.0), (r("sel"), 0.0),
                    (r("hold32", 0, 256, 32), 0.0), (r("hold16", 0, 128, 16), 0.0), (r("hold8", 0, 128, 16), 0.0), (r("hold8", 8, 128, 16), 8.0),
                    (r("rst", 0, 256, 4), LOW), (r("cb", 0, 64, 16), -1024.0), (r("cb", 64, 192, 4), 0.0)):
        op("set", view, c)
    op("ts", r15, pidx, 15, None, A.bitwise_and)
    op("ts", r31, pidx, 31, None, A.bitwise_and)
    op("ts", rq, pidx, 1, 16, A.logical_shift_right, A.bitwise_and)
    op("copy", r("ci"), r(io, 0, 128))
    op("act", r("d1"), r(io, 0, 256), CP, scale=0.0)
    op("act", r("k2"), r(io, 0, 128), CP, scale=64.0)
    op("copy", ip, r15)
    op("copy", sp31, r31)
    op("ts", r("cmod", 0, 128), r("ci"), 15, None, A.bitwise_and)
    op("ts", r("rsh"), r("ci", 0, 64), 1, None, A.logical_shift_right)
    op("ts", pc, rq, ip, None, A.add)
    op("ts", top0, ip, 0.5, BIG, A.add, A.mult)
    op("ts", spx, sp31, float(me), 99.0, A.is_equal, A.mult)
    op("ts", t8x, sp31, 8.0, 99.0, A.is_lt, A.mult)
    op("ts", t8, t8x, sp31, -8.0, A.add, A.add)
    op("ts", r("mask16"), r("cmod", 0, 128), ip, None, A.is_equal)
    op("ts", r("dupo", 0, 16), r("rsh", 0, 16), 16.0, ip, A.mult, A.add)
    op("copy", r("repo"), r("rsh"))
    op("tt", spart, spx, sp31, A.add)
    op("ts", r("mneg"), r("selr"), pc, -1024.0, A.not_equal, A.mult)

    for t in range(4):
        op("ts", r("ubig", t, 512, 4), r("ones"), r("ut", t, t + 1), None, A.mult)
    op("quant", r("uq"), r("us"), r("ubig"))
    for a in range(2):
        op("copy", r("offh", 0, 16, p=halves[a]), r("l1", 16 * a, 16 * a + 16, p=halves[a]))
        op("ts", r("zi", p=halves[a]), r("l1", 16 * a, 16 * a + 16, p=halves[a]), 7, None, A.logical_shift_right)
    op("act", r("kp"), by(r(io), r("offh", 0, 16)), CP)
    for k in range(4):
        op("tt", r("key1" if k == 3 else "em", k, 256, 4), r("kp", k, 256, 4), r("mask16", 0, 64), A.mult)
    for k in range(3):
        op("tt", r("key1", k, 256, 4), r("em", k, 256, 4), r("key1" if k == 2 else "em", k + 1, 256, 4), A.subtract)
    op("copy", r("offh", 16, 32), r("zi"))
    op("ts", r("pf", 16, 24), r(io, 0, 8), spart, None, A.is_equal)
    op("act", r("wn", 0, 256), by(r("pf", 16, 24), r("offh", 16, 32)), CP)
    op("act", r("wn", 256, 512, 4), r("wn", 1, 256, 4), CP, scale=-1.0)
    op("ts", r("cmod", 128, 192), r("ci", 0, 64), 4, None, A.logical_shift_right)
    op("ts", r("mk", 128, 192), r("cmod", 128, 192), t8, 2.0, A.is_gt, A.mult)
    op("tt", r("wn", 259, 512, 4), r("wn", 3, 256, 4), r("mk", 128, 192), A.add)
    for k in (1, 2):
        op("tt", r("wn", 256 + k, 512, 4), r("wn", k, 256, 4), r("wn", k + 1, 256, 4), A.subtract)
    op("ts", r64, pidx, 64, None, A.bitwise_and)
    op("ts", ph, r64, ip, None, A.add)
    op("ts", r("dupo", 16, 24), r("dupo", 0, 8), 4.0, 3.0, A.mult, A.add)
    op("copy", r("offo"), r("lo"))
    for a in range(2):
        op("act", rank("er2", a, 256), by(r(io), rank("offo", a, 16)), CP)
    op("scan", r("es2", 128, 192), r("hold16", 0, 64), r("em", 0, 256, 4), 0.0, A.mult, A.add)
    etab, etab2 = r("es2", 143, 192, 16), r("es2", 15, 128, 16)
    for a in range(2):
        op("tt", rank("ew2", a, 64), r("er2", 256 * a, 256 * a + 256, 4), r("mask16", 0, 64), A.mult)
    op("scan", r("es2", 0, 128), r("hold16"), r("ew2"), 0.0, A.mult, A.add)
    for i in range(4):
        op("quant", rank("aq", i), rank("asc", i), rank("at", i, 512))
    op("quant", r("wq"), r("ws"), r("wt"))

    def f8(i):
        return rank("f8", i, 8)

    def i8(i):
        return rank("i8", i, 8)

    def mm(out, w, x, behind=()):
        return op("mm", out, w[0], w[1], x[0], x[1], True, True, behind=behind)

    U = r("uq"), r("us")

    for i, s in enumerate([me] + [(me - q) % N for sem, share in tiers for q in share]):
        bank = r("ps" if i < 4 else "pr", 512 * (i % 4), 512 * (i % 4) + 128)
        mm(bank, U, (rank("hall", s), rank("halls", s)))
        if i % 2:
            op("copy", rank("sc", s), bank)
        else:
            op("act", rank("sc", s), bank, CP)

    op("copy", rank("gv", 0), by(r("sc"), r("offh", 0, 8)))
    op("act", rank("gv", 1), by(r("sc"), r("offh", 8, 16)), CP)
    for i in range(2):
        op("scan", rank("mx", i), rank("rst", i), rank("gv", i), 0.0, A.add, A.max)
        for k in (1, 2, 3):
            a, e = 128 * i + k, 128 * i + 128
            op("tt", r("pm", a, e, 4), r("gv", a, e, 4), r("mx", a - 1, e, 4), A.is_le)
        op("scan", rank("wn", 4 + i), rank("pm", i), rank("wn", 2 + i), 0.0, A.mult, A.add)
        op("scan", rank("st1", i), rank("pm", i), rank("key1", i), 0.0, A.mult, A.add)

    def spread(out, name, a, b, step, add=0.0):
        for i, to in enumerate(halves):
            for there in halves:
                op("ts", r("cu1", out + 4 * i, out + 4 * i + 4, p=there), r(name, a, b, step, to), add, None, A.add)

    chosen = r("cs", 143, 192, 16)
    op("scan", r("cs", 128, 192), r("hold16", 0, 64), r("st1", 3, 256, 4), 0.0, A.mult, A.add)
    spread(8, "cs", 143, 192, 16)
    spread(16, "es2", 143, 192, 16, -128.0 * me)
    op("act", rank("x1s", 0), by(r("halls"), r("cu1", 8, 16)), CP)
    op("copy", rank("x1", 0), by(r("hall"), r("cu1", 8, 16)))
    op("act", rank("x1s", 1), by(rank("halls", me), r("cu1", 16, 24)), CP)
    op("copy", rank("x1", 1), by(rank("hall", me), r("cu1", 16, 24)))
    op("act", r("dup1"), by(r("wn", 512, 768), r("dupo", 16, 24)), IDN, bias=1.0e6, scale=-1.0e6)
    for out in (r("cum1", 64, 128, p=halves[1]), r("cum1", 0, 64, p=halves[0])):
        op("scan", out, r("ones", 0, 64, p=halves[0]), r("wn", 515, 768, 4, halves[0]), -16.5, A.mult, A.add)
    op("scan", r("cum1", 0, 64, p=halves[1]), r("ones", 0, 64, p=halves[1]), r("wn", 515, 768, 4, halves[1]), r("cum1", 127, 128, p=halves[1]),
       A.mult, A.add)
    op("tt", r("v1"), by(r("cum1", 0, 64), r("dupo", 0, 8)), r("dup1"), A.is_gt)
    op("tr", r("vt1"), r("v1"))
    op("scan", rank("vs1", 0), r("hold8"), r("vt1"), 0.0, A.mult, A.add)
    for i, to in enumerate(halves):
        for there in halves:
            op("ts", r("cu1", 24 + 4 * i, 28 + 4 * i, p=there), r("vs1", 15, 128, 32, to), 16.0, r("pf", 8, 9, p=to), A.mult, A.add)
    op("scan", rank("vs1", 1), r("hold16"), r("vt1"), 0.0, A.mult, A.add)
    op("copy", r("sel", 1, 9, 2), chosen)
    op("tt", r("sel", 0, 8, 2), etab, chosen, A.subtract)
    op("scan", r("sel", 16, 24), r("vs1", 135, 256, 16), r("sel", 1, 9), r("sel", 0, 1), A.mult, A.add)
    spread(0, "sel", 16, 24, 2)

    def products(out, X):
        m, a = [], []
        for i in range(4):
            m = [mm(r("pr", 512 * i, 512 * i + 128), (rank("aq", i), rank("asc", i)), X, m)]
            a = [op("act", out(i), r("pr", 512 * i, 512 * i + 128), CP, behind=a, scale=0.05)]

    for h in (1, 0):
        products(lambda i: rank("hs1", 2 * i + h), (rank("x1", h), rank("x1s", h)))
    op("act", r("base1"), by(r("sc"), r("cu1", 0, 8)), CP)
    for i in range(4):
        op("tt", r("h1", i, 512, 4), by(rank("hs1", i, 256), r("cu1", 24, 32)), r("e1t", i, 512, 4), A.add)
    H1 = r("h1q"), r("h1s")
    op("quant", H1[0], H1[1], r("h1"))

    mm(r("ps", 0, 128), U, H1)
    op("tr", r("bt"), r("base1"))
    op("tr", r("gt"), r("ps", 0, 128))
    op("tt", rank("sp", me, 4), r("gt", 0, 128, 32), r("bt", 0, 128, 32), A.add)
    own_sp = T.sp[:, 4 * me:4 * me + 4]
    sent = send(far(T, topo, core, me, SCORES, "ae", lambda q: own_sp, lambda d: own_sp), [rank("sp", me, 4)])
    arrive("ae", count(SCORES), [rank("sp", s, 4) for s in range(N) if s != me], sent)
    op("tt", rank("sc2", me), r("ps", 0, 128), r("base1"), A.add)
    products(lambda i: rank("rs", 2 * i + 1), H1)
    op("act", rank("chr", 0), by(r(io), r("cu1", 0, 8)), CP)
    dma("y", ("ch", s_[0:1, :]), r("chr", 0, 128, p=slice(0, 1)), 1.2, [sent], "d23")

    op("copy", r("off2", 0, 32), r("l2"))
    op("ts", r("si"), r("l2"), 7, None, A.logical_shift_right)
    op("copy", r("off2", 32, 64), r("si"))
    op("ts", r("pf", 24, 32), r(io, 0, 8), float(me), BIG, A.is_equal, A.mult)
    for s in range(N):
        op("act", rank("wcol", s), r(io, 0, 128), CP, scale=0.5 if s == me else 0.0)
    for h in range(4):
        op("act", rank("hm2", h), by(r("pf", 24, 32), rank("off2", 4 + h, 8)), CP)
        op("act", rank("col2", h), by(r("wcol"), rank("off2", h, 8)), CP)
    op("act", r("cw2", 0, 512, 4), r("hm2", 1, 512, 4), CP, scale=-1.0)
    op("act", r("cw2", 3, 512, 4), r("hm2", 3, 512, 4), CP)
    op("act", r("col2", 0, 512, 4), r("k2"), CP)
    q0 = quarters[0]
    op("act", r("ce2", 3, 512, 4, q0), r("er2", 3, 512, 4, q0), CP)
    for h in range(2):
        a, e = 256 * h, 256 * h + 256
        for k in (1, 2):
            op("tt", r("cw2", a + k, e, 4), r("hm2", a + k, e, 4), r("hm2", a + k + 1, e, 4), A.subtract)
        for k in range(3):
            op("tt", r("ce2", a + k, e, 4, q0), r("er2", a + k, e, 4, q0), r("er2", a + k + 1, e, 4, q0), A.subtract)
    for h in range(4):
        op("scan", rank("k1", h), hold4, rank("col2", h), 0.0, A.mult, A.add)

    for q in range(1, N):
        s = (me + q) % N
        if q == 1:
            op("copy", rank("rp", s), by(r("sp"), rank("repo", s, 8)))
        elif q < 4:
            op("copy", r("d1", 128 * q - 256, 128 * q - 128, 32), rank("sp", s, 4))
            op("scan", rank("rp", s), r("hold32", 0, 128), rank("d1", q - 2), 0.0, A.mult, A.add)
        else:
            op("act", rank("rp", s), by(r("sp"), rank("repo", s, 8)), CP)
        op("tr", rank("sc2", s), rank("rp", s))

    for h in range(2):
        op("copy", rank("gw", h), by(r("sc2"), rank("off2", h, 8)))
        op("act", rank("gw", 2 + h), by(r("sc2"), rank("off2", 2 + h, 8)), CP)
    for h in (0, 2, 1, 3):
        op("scan", rank("mx2", h), r("rst", 0, 128), rank("gw", h), 0.0, A.add, A.max)
        for k in (1, 2, 3):
            a, e = 128 * h + k, 128 * h + 128
            op("tt", r("pm2", a, e, 4), r("gw", a, e, 4), r("mx2", a - 1, e, 4), A.is_le)
        op("scan", r("won2", 128 * h + 4, 128 * h + 132), rank("pm2", h), rank("cw2", h), 0.0, A.mult, A.add)
    op("scan", r("ce"), r("ones"), r("won2", 3, 512, 4), top0, A.mult, A.subtract)
    op("scan", rank("ks", 0), r("ce"), r("k1", 3, 512, 4), 0.0, A.max, A.min)
    op("scan", rank("ks", 1), r("ce"), r("k2"), 0.0, A.max, A.min)
    op("ts", r("lr"), r("mneg"), r("ks", 127, 128), r("ks", 255, 256), A.add, A.subtract)
    op("tr", r("lt"), r("lr"))
    for there in halves:
        for a, to in enumerate(halves):
            op("scan", r("ls", 64 * a, 64 * a + 64, p=there), r("cb", 0, 64, p=to), r("lt", p=to), 0.0, A.add, A.max)
    for a in range(4):
        op("tt", r("r8", p=quarters[a]), r("ls", 15, 128, 16, quarters[a]), r("ls", 15, 128, 16, quarters[a ^ 1]), A.max)
    op("ts", r("offp"), r("r8"), 2.0, None, A.mult)
    op("act", r("pks"), by(H1[1], r("offp")), CP)
    op("copy", r("pk"), by(H1[0], r("offp")))

    spans = [slice(16 * min(share), 16 * max(share) + 16) for share in PICKS_H]
    sent = send(near(T, topo, core, me, "kc", lambda i: T.pk[:, spans[i]].bitcast(dt.uint8)), [r("pk")])
    first = sent = send(near(T, topo, core, me, "ks", lambda i: T.pks[:, spans[i]]), [r("pks")], [sent])
    for share, (sem, src, dst) in zip(PICKS, pick_calls(T, me)):
        sent = send(far(T, topo, core, me, share, "a2", src, dst), [], [sent])
    arrive("a2", count(*PICKS) + 2 * count(*PICKS_H), [rank(n, s, 16) for s in range(N) if s != me for n in ("win2", "win2s")], first)

    for h in range(4):
        op("scan", r("e2s", 128 * h, 128 * h + 128, p=q0), r("pm2", 128 * h, 128 * h + 128, p=q0), r("ce2", 128 * h, 128 * h + 128, p=q0), 0.0,
           A.mult, A.add)
    op("act", r("zf2", 128, 256, p=slice(0, 1)), r("e2s", 3, 512, 4, slice(0, 1)), CP)
    op("bc", rank("zf2", 0), r("zf2", 128, 256, p=slice(0, 1)), 128)
    cnt, mk, c2 = r("vs", 31, 256, 32), r("mk", 0, 128), r("cs", 15, 128, 16)
    op("copy", r("zb2"), rank("zf2", 0))
    for h in range(2):
        op("tt", rank("base2", h, 64), rank("zf2", h, 64), r("mask16", 0, 64), A.mult)
    op("scan", r("cs", 0, 128), r("hold16"), r("base2"), 0.0, A.mult, A.add)
    op("ts", r("sj"), r("zb2"), 7, None, A.logical_shift_right)
    op("ts", mk, r("sj"), spart, None, A.is_equal)
    op("act", r("dup2"), by(mk, r("dupo", 0, 16)), CP)
    op("copy", i8(2), c2)
    op("scan", r("cum"), r("ones"), mk, 0.0, A.mult, A.add)
    op("ts", f8(4), c2, float(128 - 128 * me), None, A.add)
    op("ts", i8(3), i8(2), 7, None, A.logical_shift_right)
    op("tt", f8(5), etab2, c2, A.subtract)
    for h in range(2):
        op("tt", rank("v2", h), by(r("cum"), rank("dupo", h, 8)), rank("dup2", h), A.mult)
    op("ts", f8(6), i8(3), 16.0, -1.0, A.mult, A.add)
    op("tr", r("vt"), r("v2"))
    op("tt", f8(7), f8(6), f8(4), A.subtract)
    op("scan", r("vs"), r("hold32"), r("vt"), 0.0, A.mult, A.add)
    op("ts", f8(8), cnt, 16.5, None, A.is_gt)
    op("ts", f8(9), cnt, 0.5, None, A.is_gt)
    op("tt", f8(10), f8(7), cnt, A.add)
    op("tt", f8(12), f8(8), f8(5), A.mult)
    op("tt", f8(11), f8(9), f8(8), A.subtract)
    op("tt", f8(14), f8(12), f8(4), A.add)
    op("tt", f8(13), f8(11), f8(10), A.mult)
    op("tt", f8(16), f8(12), c2, A.add)
    op("tt", f8(15), f8(13), f8(14), A.add)
    op("copy", r("cu2"), f8(16))
    op("copy", r("ixu"), f8(15))
    op("act", r("base2"), by(r("sc2"), r("cu2")), CP)
    op("act", rank("chr", 1), by(r(io), r("cu2")), CP)
    dma("y", ("ch", s_[1:2, :]), r("chr", 128, 256, p=slice(0, 1)), 1.2, sem="d23")

    products(lambda i: rank("rs", 2 * i), (r("win2"), r("win2s")))
    for i in range(4):
        op("tt", r("h2", i, 512, 4), by(rank("rs", i, 256), r("ixu")), r("e2t", i, 512, 4), A.add)
    H2 = r("h2q"), r("h2s")
    op("quant", H2[0], H2[1], r("h2"))

    mm(r("ps", 512, 640), (r("wq"), r("ws")), H2)
    mm(r("ps", 0, 128), U, H2)
    dma("y", whole("oc"), H2[0], 1.4, sem="d23")
    for k in range(4):
        dma("ys"[k // 2], ("osc", s_[4 * k:4 * k + 4, :]), r("h2s", p=slice(32 * k, 32 * k + 4)), 1.2, sem="d23")
    op("act", r("yt"), r("ps", 512, 640), CP)
    op("tt", r("gout"), r("ps", 0, 128), r("base2"), A.add)
    dma("s", whole("y"), r("yt"), 1.4, sem="d23")
    dma("y", whole("g"), r("gout", p=slice(0, 1)), 1.2, sem="d23")

    if not ORDER:
        ORDER.extend(order(steps))
    seq = ORDER
    total, upto = {}, {}
    for i in seq:
        s = steps[i]
        total[s["sem"]] = total.get(s["sem"], 0) + s["count"]
        upto[i] = total[s["sem"]]
    total["left"] = left[0]
    known, done, waited = {q: 0 for q in Q}, {}, {}
    before = {q: 0 for q in Q}
    for i in seq:
        s = steps[i]
        q = s["q"]
        if q is None:
            done[i] = 1 << i
            continue
        for d in sorted(s["deps"], key=lambda d: -seq.index(d)):
            t = steps[d]
            if known[q] >> d & 1:
                continue
            n = upto[d] if t["sem"][0] == "q" else total[t["sem"]]
            if waited.get((q, t["sem"]), 0) < n:
                Q[q].wait_ge(T.sem[t["sem"]], n)
                waited[q, t["sem"]] = n
            known[q] |= done[d]
        ins = s["call"]()
        if s["count"]:
            ins.then_inc(T.sem[s["sem"]], s["count"])
        done[i] = known[q] | 1 << i
        if s["sem"][0] == "q":
            done[i] |= before[q]
            before[q] = done[i]
    for sem in sorted(total):
        if all(waited.get((q, sem), 0) < total[sem] for q in Q):
            g.wait_ge(T.sem[sem], total[sem])
